import numpy as np
import ml_dtypes


def mxq(x, axis, fmt="e4m3"):
    dtype, down = {"e4m3": (ml_dtypes.float8_e4m3fn, 7), "e5m2": (ml_dtypes.float8_e5m2, 14)}[fmt]
    v = np.moveaxis(np.asarray(x, np.float32).astype(ml_dtypes.bfloat16).astype(np.float64), axis, -1)
    blocks = v.reshape(v.shape[:-1] + (-1, 32))
    amax = np.abs(blocks).max(-1, keepdims=True)
    byte = np.maximum(np.where(amax > 0, np.frexp(amax)[1] - 1 + 127, 0) - down, 1)
    scale = np.exp2(byte - 127.0)
    codes = (blocks / scale).astype(np.float32).astype(dtype).astype(np.float64)
    return np.moveaxis((codes * scale).reshape(v.shape), -1, axis)


WIDE = False


def mx_kscale(k):
    if not WIDE:
        return np.ones(k)
    levels = np.array([10, -10, 5, -5, 0])
    if k % 512:
        return np.exp2(np.random.permutation(np.resize(levels, k // 32))).repeat(32)
    a = np.empty((k // 512, 16))
    for p in range(k // 512):
        a[p, :8] = np.random.permutation(np.resize(levels, 8))
        for g in range(8):
            far = levels[np.abs(levels - a[p, g]) >= 10]
            a[p, g + 8] = far[np.random.randint(len(far))]
    return np.exp2(a.ravel()).repeat(32)


def f64(x):
    return np.asarray(x).astype(np.float64)


def striped(idx):
    return np.tile(np.asarray(idx).reshape(-1, 16).T, (8, 1)).astype(np.uint16)


def unstriped(offs):
    return offs[:16].T.reshape(-1).astype(np.int64)


E2M1 = np.array([0.0, 0.5, 1.0, 1.5, 2.0, 3.0, 4.0, 6.0, -0.0, -0.5, -1.0, -1.5, -2.0, -3.0, -4.0, -6.0])


def pack_weight(w, fmt):
    k, n = w.shape
    w = f64(np.asarray(w, np.float32).astype(ml_dtypes.bfloat16)).reshape(k // 32, 32, n)
    amax = np.abs(w).max(1)
    if fmt == "e4m3":
        byte = np.frexp(amax)[1] - 1 + 127 - 7
    else:
        mant, ex = np.frexp(amax / 6.0)
        byte = np.where(mant > 0.5, ex, ex - 1) + 127
    byte = np.clip(np.where(amax > 0, byte, 1), 1, 254)
    scaled = (w * np.exp2(127.0 - byte)[:, None, :]).reshape(k, n).astype(np.float32)
    by_word = np.ascontiguousarray(scaled.reshape(k // 512, 128, 4, n).transpose(0, 1, 3, 2))
    if fmt == "e4m3":
        words = by_word.astype(ml_dtypes.float8_e4m3fn).view(np.uint8)
    else:
        c = by_word.astype(ml_dtypes.float4_e2m1fn).view(np.uint8) & 0xF
        words = (c[..., 0::2] | (c[..., 1::2] << 4)).reshape(k // 512, 128, 2 * n)
    return np.ascontiguousarray(words), np.ascontiguousarray(byte.astype(np.uint8).reshape(k // 512, 16, n))


def unpack_weight(words, scales, fmt):
    g, _, n = scales.shape
    words = np.ascontiguousarray(words).reshape(g, 128, n, -1)
    if fmt == "e4m3":
        vals = words.view(ml_dtypes.float8_e4m3fn).astype(np.float64)
    else:
        nib = np.empty((g, 128, n, 4), np.uint8)
        nib[..., 0::2] = words & 0xF
        nib[..., 1::2] = words >> 4
        vals = E2M1[nib]
    vals = vals * np.repeat(np.exp2(scales.astype(np.float64) - 127.0), 8, axis=1)[..., None]
    return vals.transpose(0, 1, 3, 2).reshape(g * 512, n)


def silu(v):
    return v / (1.0 + np.exp(-v))


def sigmoid(v):
    return 1.0 / (1.0 + np.exp(-v))


D, T, I, Q, U = 512, 1024, 256, 512, 1024


def setup_inputs():
    n = np.random.standard_normal
    idx = np.random.permutation(T)[:I]
    idx2 = np.random.permutation(T)[:I]
    idx4 = np.random.permutation(U)[:Q]
    fd = mx_kscale(D)
    fq = mx_kscale(Q)
    qpoolp = pack_weight(n((D, U)) * 0.03 * fd[:, None], "e4m3")
    return {
        "keys": (n((D, T))).astype(np.float32),
        "qpool_words": qpoolp[0],
        "qpool_scales": qpoolp[1],
        "ksc": (np.random.uniform(0.5, 2.0, (D, 1)) / fd[:, None]).astype(np.float32),
        "qs": (np.random.uniform(16.0, 64.0, (Q, 1)) * fq[:, None]).astype(np.float32),
        "target": (np.random.uniform(0.0, 0.008, (Q, I))).astype(np.float32),
        "qrows": (n((Q, D)) / fq[:, None]).astype(np.float32),
        "fr": (np.random.uniform(0.2, 0.8, (1, I))).astype(np.float32),
        "sg": (np.random.uniform(0.5, 2.0, (1, I))).astype(np.float32),
        "old": (n((D, T)) * 1.0).astype(np.float32),
        "fade": (np.random.uniform(0.5, 1.0, (1, T))).astype(np.float32),
        "offs": striped(idx),
        "offs2": striped(idx2),
        "offs4": striped(idx4),
    }


def reference(keys, qpool_words, qpool_scales, ksc, qs, target, qrows, fr, sg, old, fade, offs, offs2, offs4):
    idx = unstriped(offs)
    idx2 = unstriped(offs2)
    idx4 = unstriped(offs4)
    qpoolu = unpack_weight(qpool_words, qpool_scales, "e4m3")
    x1 = f64(keys)[:, idx] * (1.0 - f64(fr)) + f64(keys)[:, idx2] * f64(fr)
    vp = silu(x1)
    kp = vp * f64(ksc)
    qpoolidx4g = qpoolu[:, idx4]
    kpq = mxq(kp, 0, "e4m3")
    a = qpoolidx4g.T @ kpq
    p = np.exp(a - np.max(a, axis=1, keepdims=True))
    ds = (p / np.sum(p, axis=1, keepdims=True) - f64(target)) * f64(qs)
    qrowsq = mxq(f64(qrows), 0, "e4m3")
    dsq = mxq(ds, 0, "e4m3")
    c0 = qrowsq.T @ dsq
    dx1 = c0 * sigmoid(x1) * (1.0 + x1 * (1.0 - sigmoid(x1)))
    gs = dx1 * f64(sg)
    gf = np.zeros((D, T))
    gf[:, idx] = gs
    y = f64(old) * f64(fade) + gf
    return y

@@ -1,0 +1,251 @@
+from contextlib import ExitStack
+
+import concourse.mybir as mybir
+from concourse.masks import make_identity
+
+D, T, I, Q, U = 512, 1024, 256, 512, 1024
+FLOPS = 2 * Q * I * D + 2 * D * I * Q
+
+F32 = mybir.dt.float32
+BF16 = mybir.dt.bfloat16
+I32 = mybir.dt.int32
+U32 = mybir.dt.uint32
+U16 = mybir.dt.uint16
+U8 = mybir.dt.uint8
+FP8X4 = mybir.dt.float8_e4m3fn_x4
+ACT = mybir.ActivationFunctionType
+ALU = mybir.AluOpType
+AXIS = mybir.AxisListType
+
+P = 128
+PACK = 4
+BANK = 512
+HALVES = I // P
+CHUNKS = T // P
+
+
+def tile_attend_bkbetween_s_kernel(tc, keys, qpool_words, qpool_scales, ksc, qs, target, qrows, fr, sg, old, fade, offs, offs2, offs4, out):
+    nc = tc.nc
+    with ExitStack() as ctx:
+        sb = ctx.enter_context(tc.tile_pool(name="sb", bufs=1))
+        ps = ctx.enter_context(tc.psum_pool(name="ps", bufs=1))
+
+        def bank(b):
+            return ps.tile([P, BANK], F32, name="bank%d" % b)
+
+        list1 = sb.tile([P, I // 16], U16, name="list1")
+        list2 = sb.tile([P, I // 16], U16, name="list2")
+        list4 = sb.tile([P, Q // 16], U16, name="list4")
+        key_planes = [sb.tile([P, T], F32, name="keys%d" % t) for t in range(PACK)]
+        fr_rows = sb.tile([P, I], F32, name="fr_rows")
+        ksc_cols = sb.tile([P, PACK], F32, name="ksc_cols")
+        qs_cols = sb.tile([P, PACK], F32, name="qs_cols")
+        pool_words = sb.tile([P, U], U32, name="pool_words")
+        pool_scales = sb.tile([P, U], U8, name="pool_scales")
+        rows = sb.tile([P, P], F32, name="rows")
+        qrows_raw = sb.tile([P, PACK, D], F32, name="qrows_raw")
+        target_raw = sb.tile([P, PACK, I], F32, name="target_raw")
+        old_halves = [sb.tile([P, PACK, BANK], F32, name="old%d" % h) for h in range(2)]
+        ident = sb.tile([P, P], F32, name="ident")
+        placed = [sb.tile([P, T], F32, name="placed%d" % t) for t in range(PACK)]
+
+        nc.vector.memset(pool_scales[:].bitcast(I32), 0)
+        nc.vector.memset(rows[:], 0.0)
+        make_identity(nc, ident[:])
+        for t in range(PACK):
+            nc.vector.memset(placed[t][:], 0.0)
+
+        keys_v = keys.rearrange("(p t) n -> t p n", t=PACK)
+        nc.sync.dma_start(list2[:], offs2)
+        nc.sync.dma_start(key_planes[0][:], keys_v[0])
+        nc.sync.dma_start(fr_rows[:], fr[0].partition_broadcast(P))
+        nc.sync.dma_start(list1[:], offs)
+        for t in range(1, PACK):
+            nc.sync.dma_start(key_planes[t][:], keys_v[t])
+        nc.sync.dma_start(pool_words[:].bitcast(I32), qpool_words[0].rearrange("p n t -> p (n t)").bitcast(I32))
+        nc.sync.dma_start(ksc_cols[:], ksc.rearrange("(p t) o -> p (t o)", t=PACK))
+        nc.sync.dma_start(list4[:], offs4)
+        nc.sync.dma_start(qrows_raw[:], qrows.rearrange("(p r) d -> p r d", r=PACK))
+        for g in range(4):
+            nc.sync.dma_start(pool_scales[32 * g : 32 * g + 4, :].bitcast(I32), qpool_scales[0, 4 * g : 4 * g + 4, :].bitcast(I32))
+        nc.sync.dma_start(target_raw[:], target.rearrange("(p r) i -> p r i", r=PACK))
+        nc.sync.dma_start(rows[0:CHUNKS, :], fade.rearrange("o (c p) -> (o c) p", p=P))
+        nc.sync.dma_start(rows[CHUNKS : CHUNKS + HALVES, :], sg.rearrange("o (h p) -> (o h) p", p=P))
+        nc.sync.dma_start(qs_cols[:], qs.rearrange("(p r) o -> p (r o)", r=PACK))
+        old_v = old.rearrange("(p t) n -> p t n", t=PACK)
+        for h in range(2):
+            nc.sync.dma_start(old_halves[h][:], old_v[:, :, h * BANK : (h + 1) * BANK])
+
+        keep_rows = sb.tile([P, I], F32, name="keep_rows")
+        nc.vector.tensor_scalar(keep_rows[:], fr_rows[:], -1.0, 1.0, ALU.mult, ALU.add)
+        silu_t = sb.tile([P, PACK, HALVES, P], F32, name="silu_t")
+        tanh_t = sb.tile([P, PACK, HALVES, P], F32, name="tanh_t")
+        kp_planes = sb.tile([P, PACK, I], BF16, name="kp_planes")
+        mix_banks = []
+        for t in range(PACK):
+            second = sb.tile([P, I], F32, name="second%d" % t)
+            first = sb.tile([P, I], F32, name="first%d" % t)
+            nc.vector.tensor_tensor(second[:], key_planes[t][:].indirect(list2[:]), fr_rows[:], ALU.mult)
+            nc.vector.tensor_tensor(first[:], key_planes[t][:].indirect(list1[:]), keep_rows[:], ALU.mult)
+            mix = bank(t)
+            mix_banks.append(mix)
+            for h in range(HALVES):
+                cols = slice(h * P, (h + 1) * P)
+                nc.tensor.matmul(mix[:, cols], second[:, cols], ident[:], start=True, stop=False, is_transpose=True)
+                nc.tensor.matmul(mix[:, cols], first[:, cols], ident[:], start=False, stop=True, is_transpose=True)
+            nc.scalar.activation(silu_t[:, t].rearrange("p h m -> p (h m)"), mix[:, 0:I], ACT.Silu)
+            for h in range(HALVES):
+                nc.tensor.transpose(mix[:, I + h * P : I + (h + 1) * P], silu_t[:, t, h, :], ident[:])
+            nc.scalar.activation(kp_planes[:, t, :], mix[:, I : 2 * I], ACT.Copy, scale=ksc_cols[:, t : t + 1])
+
+        q_words = sb.tile([P, PACK, P], U32, name="q_words", align_bytes=64)
+        nc.vector.tensor_copy(q_words[:].rearrange("p r s -> p s r"), pool_words[:].indirect(list4[:]))
+        q_bytes = sb.tile([P, Q], U8, name="q_bytes")
+        nc.vector.tensor_copy(q_bytes[:], pool_scales[:].indirect(list4[:]))
+        q_scales = sb.tile([P, PACK, P], U8, name="q_scales", align_bytes=64)
+        nc.vector.tensor_copy(q_scales[:].rearrange("p r s -> p s r"), q_bytes[:].rearrange("p (s r) -> p s r", r=PACK))
+
+        kp_woven = sb.tile([P, I, PACK], BF16, name="kp_woven", align_bytes=64)
+        nc.vector.tensor_copy(
+            kp_woven[:].rearrange("p (c e) t -> p c t e", e=4), kp_planes[:].rearrange("p t (c e) -> p c t e", e=4)
+        )
+        kp_words = sb.tile([P, I], U32, name="kp_words", align_bytes=64)
+        kp_scales = sb.tile([P, I], U8, name="kp_scales", align_bytes=64)
+        nc.vector.quantize_mx(out=kp_words[:].bitcast(FP8X4), scales=kp_scales[:], in_=kp_woven[:].rearrange("p i t -> p (i t)"))
+
+        score_banks = [bank(4), bank(5)]
+        for r in range(PACK):
+            nc.tensor.matmul_mx(
+                out=score_banks[r // 2][:, (r % 2) * I : (r % 2 + 1) * I],
+                lhsT=q_words[:, r, :].bitcast(FP8X4),
+                lhsT_scale=q_scales[:, r, :],
+                rhs=kp_words[:].bitcast(FP8X4),
+                rhs_scale=kp_scales[:],
+                start=True,
+                stop=True,
+            )
+
+        qrows_woven = sb.tile([P, PACK, P, PACK], BF16, name="qrows_woven", align_bytes=64)
+        for c in range(4):
+            ms = slice(c * 32, (c + 1) * 32)
+            nc.scalar.copy(
+                qrows_woven[:, :, ms, :].rearrange("p j m r -> p m r j"),
+                qrows_raw[:].rearrange("p r (m j) -> p m r j", j=PACK)[:, ms],
+            )
+        qrows_words = sb.tile([P, D], U32, name="qrows_words", align_bytes=64)
+        qrows_scales = sb.tile([P, D], U8, name="qrows_scales", align_bytes=64)
+        nc.vector.quantize_mx(
+            out=qrows_words[:].bitcast(FP8X4), scales=qrows_scales[:], in_=qrows_woven[:].rearrange("p j m r -> p (j m r)")
+        )
+
+        turned = bank(6)
+        nc.tensor.transpose(turned[:, 0:P], rows[:], ident[:])
+        cols_sb = sb.tile([P, 16], F32, name="cols_sb")
+        nc.scalar.copy(cols_sb[:], turned[:, 0:16])
+        half_sg = sb.tile([P, HALVES], F32, name="half_sg")
+        nc.scalar.activation(half_sg[:], turned[:, CHUNKS : CHUNKS + HALVES], ACT.Copy, scale=0.5)
+
+        for t in range(PACK):
+            nc.scalar.activation(tanh_t[:, t].rearrange("p h m -> p (h m)"), mix_banks[t][:, 0:I], ACT.Tanh, scale=-0.5)
+        gain_t = sb.tile([P, PACK, HALVES, P], F32, name="gain_t")
+        for h in range(HALVES):
+            nc.scalar.activation(
+                gain_t[:, :, h, :], tanh_t[:, :, h, :], ACT.Identity, bias=half_sg[:, h : h + 1], scale=half_sg[:, h : h + 1]
+            )
+
+        scaled_target = sb.tile([P, PACK, I], F32, name="scaled_target")
+        for r in range(PACK):
+            nc.scalar.activation(scaled_target[:, r, :], target_raw[:, r, :], ACT.Copy, scale=qs_cols[:, r : r + 1])
+
+        neg_max = [sb.tile([P, 2], F32, name="neg_max%d" % b) for b in range(2)]
+        sums = [sb.tile([P, 2], F32, name="sums%d" % b) for b in range(2)]
+        probs = sb.tile([P, PACK, I], F32, name="probs")
+        for b in range(2):
+            nc.vector.tensor_reduce(
+                neg_max[b][:], score_banks[b][:].rearrange("p (r i) -> p r i", r=2), AXIS.X, ALU.max, negate=True
+            )
+        for r in range(PACK):
+            nc.scalar.activation(
+                probs[:, r, :],
+                score_banks[r // 2][:, (r % 2) * I : (r % 2 + 1) * I],
+                ACT.Exp,
+                bias=neg_max[r // 2][:, r % 2 : r % 2 + 1],
+                accum_out=sums[r // 2][:, r % 2 : r % 2 + 1],
+            )
+
+        slope_t = sb.tile([P, PACK, HALVES, P], F32, name="slope_t")
+        nc.vector.scalar_tensor_tensor(
+            slope_t[:].rearrange("p t h m -> p (t h m)"),
+            silu_t[:].rearrange("p t h m -> p (t h m)"),
+            -1.0,
+            gain_t[:].rearrange("p t h m -> p (t h m)"),
+            ALU.add,
+            ALU.mult,
+        )
+
+        ds_planes = sb.tile([P, PACK, I], BF16, name="ds_planes")
+        for b in range(2):
+            inv = sb.tile([P, 2], F32, name="inv%d" % b)
+            nc.vector.reciprocal(inv[:], sums[b][:])
+            row_scale = sb.tile([P, 2], F32, name="row_scale%d" % b)
+            nc.vector.tensor_tensor(row_scale[:], inv[:], qs_cols[:, 2 * b : 2 * b + 2], ALU.mult)
+            for e in range(2):
+                r = 2 * b + e
+                nc.vector.scalar_tensor_tensor(
+                    ds_planes[:, r, :], probs[:, r, :], row_scale[:, e : e + 1], scaled_target[:, r, :], ALU.mult, ALU.subtract
+                )
+        ds_woven = sb.tile([P, I, PACK], BF16, name="ds_woven", align_bytes=64)
+        nc.vector.tensor_copy(
+            ds_woven[:].rearrange("p (c e) r -> p c r e", e=4), ds_planes[:].rearrange("p r (c e) -> p c r e", e=4)
+        )
+        ds_words = sb.tile([P, I], U32, name="ds_words", align_bytes=64)
+        ds_scales = sb.tile([P, I], U8, name="ds_scales", align_bytes=64)
+        nc.vector.quantize_mx(out=ds_words[:].bitcast(FP8X4), scales=ds_scales[:], in_=ds_woven[:].rearrange("p i r -> p (i r)"))
+
+        factor = [sb.tile([P, I], F32, name="factor%d" % t) for t in range(PACK)]
+        for t in range(PACK):
+            for h in range(HALVES):
+                dst = mix_banks[t][:, I + h * P : I + (h + 1) * P]
+                nc.tensor.matmul(dst, slope_t[:, t, h, :], ident[:], start=True, stop=False, is_transpose=True)
+                nc.tensor.matmul(
+                    dst, cols_sb[:, CHUNKS + h : CHUNKS + h + 1].to_broadcast([P, P]), ident[:], start=False, stop=True, is_transpose=True
+                )
+            nc.scalar.copy(factor[t][:], mix_banks[t][:, I : 2 * I])
+
+        grad_banks = [bank(4), bank(5)]
+        grads = [sb.tile([P, I], F32, name="grad%d" % t) for t in range(PACK)]
+        for t in range(PACK):
+            nc.tensor.matmul_mx(
+                out=grad_banks[t // 2][:, (t % 2) * I : (t % 2 + 1) * I],
+                lhsT=qrows_words[:, t * P : (t + 1) * P].bitcast(FP8X4),
+                lhsT_scale=qrows_scales[:, t * P : (t + 1) * P],
+                rhs=ds_words[:].bitcast(FP8X4),
+                rhs_scale=ds_scales[:],
+                start=True,
+                stop=True,
+            )
+        for t in range(PACK):
+            nc.scalar.copy(grads[t][:], grad_banks[t // 2][:, (t % 2) * I : (t % 2 + 1) * I])
+        for t in range(PACK):
+            nc.vector.tensor_tensor(placed[t][:].indirect(list1[:]), grads[t][:], factor[t][:], ALU.mult)
+
+        faded_t = []
+        for c in range(CHUNKS):
+            turned = bank(6 + c % 2)
+            for t in range(PACK):
+                nc.tensor.transpose(
+                    turned[:, t * P : (t + 1) * P], old_halves[c // 4][:, t, (c % 4) * P : (c % 4 + 1) * P], ident[:]
+                )
+            piece = sb.tile([P, PACK, P], F32, name="faded%d" % c)
+            nc.scalar.activation(piece[:].rearrange("p t m -> p (t m)"), turned[:], ACT.Copy, scale=cols_sb[:, c : c + 1])
+            faded_t.append(piece)
+
+        out_v = out.rearrange("(p t) n -> t p n", t=PACK)
+        for t in range(PACK):
+            for h in range(2):
+                back = bank((2 * t + h) % 4)
+                for e in range(4):
+                    nc.tensor.transpose(back[:, e * P : (e + 1) * P], faded_t[4 * h + e][:, t, :], ident[:])
+                result = sb.tile([P, BANK], F32, name="result%d_%d" % (t, h))
+                nc.vector.tensor_tensor(result[:], back[:], placed[t][:, h * BANK : (h + 1) * BANK], ALU.add)
+                nc.sync.dma_start(out_v[t][:, h * BANK : (h + 1) * BANK], result[:])

@@ -43,72 +43,94 @@ def tile_attend_bkbetween_s_kernel(tc, keys, qpool_words, qpool_scales, ksc, qs,
         pool_words = sb.tile([P, U], U32, name="pool_words")
         pool_scales = sb.tile([P, U], U8, name="pool_scales")
         rows = sb.tile([P, P], F32, name="rows")
-        qrows_raw = sb.tile([P, PACK, D], F32, name="qrows_raw")
+        qrows_raw = [sb.tile([P, PACK, D // 2], F32, name="qrows_raw%d" % h) for h in range(2)]
         target_raw = sb.tile([P, PACK, I], F32, name="target_raw")
         old_halves = [sb.tile([P, PACK, BANK], F32, name="old%d" % h) for h in range(2)]
         ident = sb.tile([P, P], F32, name="ident")
         placed = [sb.tile([P, T], F32, name="placed%d" % t) for t in range(PACK)]
 
-        nc.vector.memset(pool_scales[:].bitcast(I32), 0)
+        nc.gpsimd.memset(pool_scales[:].bitcast(I32), 0)
         nc.vector.memset(rows[:], 0.0)
         make_identity(nc, ident[:])
         for t in range(PACK):
             nc.vector.memset(placed[t][:], 0.0)
 
         keys_v = keys.rearrange("(p t) n -> t p n", t=PACK)
+        qrows_v = qrows.rearrange("(p r) d -> p r d", r=PACK)
+        nc.sync.dma_start(list4[:], offs4)
         nc.sync.dma_start(list2[:], offs2)
         nc.sync.dma_start(key_planes[0][:], keys_v[0])
         nc.sync.dma_start(fr_rows[:], fr[0].partition_broadcast(P))
-        nc.sync.dma_start(list1[:], offs)
-        for t in range(1, PACK):
-            nc.sync.dma_start(key_planes[t][:], keys_v[t])
-        nc.sync.dma_start(pool_words[:].bitcast(I32), qpool_words[0].rearrange("p n t -> p (n t)").bitcast(I32))
-        nc.sync.dma_start(ksc_cols[:], ksc.rearrange("(p t) o -> p (t o)", t=PACK))
-        nc.sync.dma_start(list4[:], offs4)
-        nc.sync.dma_start(qrows_raw[:], qrows.rearrange("(p r) d -> p r d", r=PACK))
         for g in range(4):
-            nc.sync.dma_start(pool_scales[32 * g : 32 * g + 4, :].bitcast(I32), qpool_scales[0, 4 * g : 4 * g + 4, :].bitcast(I32))
-        nc.sync.dma_start(target_raw[:], target.rearrange("(p r) i -> p r i", r=PACK))
+            nc.scalar.dma_start(pool_scales[32 * g : 32 * g + 4, :].bitcast(I32), qpool_scales[0, 4 * g : 4 * g + 4, :].bitcast(I32))
+        nc.sync.dma_start(list1[:], offs)
+        nc.sync.dma_start(key_planes[1][:], keys_v[1])
+        nc.sync.dma_start(qrows_raw[0][:], qrows_v[:, :, 0 : D // 2])
+        nc.sync.dma_start(key_planes[2][:], keys_v[2])
         nc.sync.dma_start(rows[0:CHUNKS, :], fade.rearrange("o (c p) -> (o c) p", p=P))
         nc.sync.dma_start(rows[CHUNKS : CHUNKS + HALVES, :], sg.rearrange("o (h p) -> (o h) p", p=P))
+        nc.sync.dma_start(key_planes[3][:], keys_v[3])
+        nc.sync.dma_start(qrows_raw[1][:], qrows_v[:, :, D // 2 : D])
+        nc.sync.dma_start(pool_words[:].bitcast(I32), qpool_words[0].rearrange("p n t -> p (n t)").bitcast(I32))
+        nc.sync.dma_start(ksc_cols[:], ksc.rearrange("(p t) o -> p (t o)", t=PACK))
+        nc.sync.dma_start(target_raw[:], target.rearrange("(p r) i -> p r i", r=PACK))
         nc.sync.dma_start(qs_cols[:], qs.rearrange("(p r) o -> p (r o)", r=PACK))
         old_v = old.rearrange("(p t) n -> p t n", t=PACK)
         for h in range(2):
             nc.sync.dma_start(old_halves[h][:], old_v[:, :, h * BANK : (h + 1) * BANK])
 
+        q_bytes = sb.tile([P, Q], U8, name="q_bytes", align_bytes=64)
+        nc.vector.tensor_copy(q_bytes[:], pool_scales[:].indirect(list4[:]))
+        q_scales = sb.tile([P, PACK, P], U8, name="q_scales", align_bytes=64)
+        nc.vector.tensor_copy(q_scales[:].rearrange("p r s -> p s r"), q_bytes[:].rearrange("p (s r) -> p s r", r=PACK))
+
         keep_rows = sb.tile([P, I], F32, name="keep_rows")
         nc.vector.tensor_scalar(keep_rows[:], fr_rows[:], -1.0, 1.0, ALU.mult, ALU.add)
         silu_t = sb.tile([P, PACK, HALVES, P], F32, name="silu_t")
         tanh_t = sb.tile([P, PACK, HALVES, P], F32, name="tanh_t")
-        kp_planes = sb.tile([P, PACK, I], BF16, name="kp_planes")
-        mix_banks = []
+        mix_banks = [bank(0), bank(1)]
+        silu_banks = [bank(2), bank(3)]
+        qrows_woven = sb.tile([P, PACK, P, PACK], BF16, name="qrows_woven", align_bytes=64)
         for t in range(PACK):
             second = sb.tile([P, I], F32, name="second%d" % t)
             first = sb.tile([P, I], F32, name="first%d" % t)
             nc.vector.tensor_tensor(second[:], key_planes[t][:].indirect(list2[:]), fr_rows[:], ALU.mult)
             nc.vector.tensor_tensor(first[:], key_planes[t][:].indirect(list1[:]), keep_rows[:], ALU.mult)
-            mix = bank(t)
-            mix_banks.append(mix)
+            mix = mix_banks[t % 2][:, (t // 2) * I : (t // 2 + 1) * I]
             for h in range(HALVES):
                 cols = slice(h * P, (h + 1) * P)
                 nc.tensor.matmul(mix[:, cols], second[:, cols], ident[:], start=True, stop=False, is_transpose=True)
                 nc.tensor.matmul(mix[:, cols], first[:, cols], ident[:], start=False, stop=True, is_transpose=True)
-            nc.scalar.activation(silu_t[:, t].rearrange("p h m -> p (h m)"), mix[:, 0:I], ACT.Silu)
+            nc.scalar.activation(silu_t[:, t].rearrange("p h m -> p (h m)"), mix, ACT.Silu)
+            nc.scalar.activation(tanh_t[:, t].rearrange("p h m -> p (h m)"), mix, ACT.Tanh, scale=-0.5)
             for h in range(HALVES):
-                nc.tensor.transpose(mix[:, I + h * P : I + (h + 1) * P], silu_t[:, t, h, :], ident[:])
-            nc.scalar.activation(kp_planes[:, t, :], mix[:, I : 2 * I], ACT.Copy, scale=ksc_cols[:, t : t + 1])
+                nc.tensor.transpose(silu_banks[h][:, t * P : (t + 1) * P], silu_t[:, t, h, :], ident[:])
+            if t in (1, 2):
+                for c in range(2):
+                    m0 = (t - 1) * 64 + c * 32
+                    nc.scalar.copy(
+                        qrows_woven[:, :, m0 : m0 + 32, :].rearrange("p j m r -> p m r j"),
+                        qrows_raw[t - 1][:].rearrange("p r (m j) -> p m r j", j=PACK)[:, c * 32 : (c + 1) * 32],
+                    )
+
+        turned = bank(6)
+        nc.tensor.transpose(turned[:, 0:P], rows[:], ident[:])
+        cols_sb = sb.tile([P, 16], F32, name="cols_sb")
+        nc.scalar.copy(cols_sb[:], turned[:, 0:16])
+        half_sg = sb.tile([P, HALVES], F32, name="half_sg")
+        nc.scalar.activation(half_sg[:], turned[:, CHUNKS : CHUNKS + HALVES], ACT.Copy, scale=0.5)
 
         q_words = sb.tile([P, PACK, P], U32, name="q_words", align_bytes=64)
         nc.vector.tensor_copy(q_words[:].rearrange("p r s -> p s r"), pool_words[:].indirect(list4[:]))
-        q_bytes = sb.tile([P, Q], U8, name="q_bytes")
-        nc.vector.tensor_copy(q_bytes[:], pool_scales[:].indirect(list4[:]))
-        q_scales = sb.tile([P, PACK, P], U8, name="q_scales", align_bytes=64)
-        nc.vector.tensor_copy(q_scales[:].rearrange("p r s -> p s r"), q_bytes[:].rearrange("p (s r) -> p s r", r=PACK))
 
         kp_woven = sb.tile([P, I, PACK], BF16, name="kp_woven", align_bytes=64)
-        nc.vector.tensor_copy(
-            kp_woven[:].rearrange("p (c e) t -> p c t e", e=4), kp_planes[:].rearrange("p t (c e) -> p c t e", e=4)
-        )
+        for h in range(HALVES):
+            nc.vector.tensor_tensor(
+                kp_woven[:, h * P : (h + 1) * P, :],
+                silu_banks[h][:].rearrange("p (t s) -> p s t", t=PACK),
+                ksc_cols[:].unsqueeze(1).to_broadcast([P, P, PACK]),
+                ALU.mult,
+            )
         kp_words = sb.tile([P, I], U32, name="kp_words", align_bytes=64)
         kp_scales = sb.tile([P, I], U8, name="kp_scales", align_bytes=64)
         nc.vector.quantize_mx(out=kp_words[:].bitcast(FP8X4), scales=kp_scales[:], in_=kp_woven[:].rearrange("p i t -> p (i t)"))
@@ -125,37 +147,25 @@ def tile_attend_bkbetween_s_kernel(tc, keys, qpool_words, qpool_scales, ksc, qs,
                 stop=True,
             )
 
-        qrows_woven = sb.tile([P, PACK, P, PACK], BF16, name="qrows_woven", align_bytes=64)
-        for c in range(4):
-            ms = slice(c * 32, (c + 1) * 32)
-            nc.scalar.copy(
-                qrows_woven[:, :, ms, :].rearrange("p j m r -> p m r j"),
-                qrows_raw[:].rearrange("p r (m j) -> p m r j", j=PACK)[:, ms],
-            )
-        qrows_words = sb.tile([P, D], U32, name="qrows_words", align_bytes=64)
-        qrows_scales = sb.tile([P, D], U8, name="qrows_scales", align_bytes=64)
-        nc.vector.quantize_mx(
-            out=qrows_words[:].bitcast(FP8X4), scales=qrows_scales[:], in_=qrows_woven[:].rearrange("p j m r -> p (j m r)")
-        )
-
-        turned = bank(6)
-        nc.tensor.transpose(turned[:, 0:P], rows[:], ident[:])
-        cols_sb = sb.tile([P, 16], F32, name="cols_sb")
-        nc.scalar.copy(cols_sb[:], turned[:, 0:16])
-        half_sg = sb.tile([P, HALVES], F32, name="half_sg")
-        nc.scalar.activation(half_sg[:], turned[:, CHUNKS : CHUNKS + HALVES], ACT.Copy, scale=0.5)
-
-        for t in range(PACK):
-            nc.scalar.activation(tanh_t[:, t].rearrange("p h m -> p (h m)"), mix_banks[t][:, 0:I], ACT.Tanh, scale=-0.5)
-        gain_t = sb.tile([P, PACK, HALVES, P], F32, name="gain_t")
+        gain_t = sb.tile([P, PACK, HALVES, P], F32, name="gain_t", align_bytes=64)
         for h in range(HALVES):
             nc.scalar.activation(
                 gain_t[:, :, h, :], tanh_t[:, :, h, :], ACT.Identity, bias=half_sg[:, h : h + 1], scale=half_sg[:, h : h + 1]
             )
 
-        scaled_target = sb.tile([P, PACK, I], F32, name="scaled_target")
+        scaled_target = sb.tile([P, PACK, I], F32, name="scaled_target", tag="tanh_t")
         for r in range(PACK):
             nc.scalar.activation(scaled_target[:, r, :], target_raw[:, r, :], ACT.Copy, scale=qs_cols[:, r : r + 1])
+
+        slope_t = sb.tile([P, PACK, HALVES, P], F32, name="slope_t", tag="kp_woven", align_bytes=64)
+        nc.vector.scalar_tensor_tensor(
+            slope_t[:].rearrange("p t h m -> p (t h m)"),
+            silu_t[:].rearrange("p t h m -> p (t h m)"),
+            -1.0,
+            gain_t[:].rearrange("p t h m -> p (t h m)"),
+            ALU.add,
+            ALU.mult,
+        )
 
         neg_max = [sb.tile([P, 2], F32, name="neg_max%d" % b) for b in range(2)]
         sums = [sb.tile([P, 2], F32, name="sums%d" % b) for b in range(2)]
@@ -164,6 +174,11 @@ def tile_attend_bkbetween_s_kernel(tc, keys, qpool_words, qpool_scales, ksc, qs,
             nc.vector.tensor_reduce(
                 neg_max[b][:], score_banks[b][:].rearrange("p (r i) -> p r i", r=2), AXIS.X, ALU.max, negate=True
             )
+        qrows_words = sb.tile([P, D], U32, name="qrows_words", tag="gain_t", align_bytes=64)
+        qrows_scales = sb.tile([P, D], U8, name="qrows_scales", align_bytes=64)
+        nc.vector.quantize_mx(
+            out=qrows_words[:].bitcast(FP8X4), scales=qrows_scales[:], in_=qrows_woven[:].rearrange("p j m r -> p (j m r)")
+        )
         for r in range(PACK):
             nc.scalar.activation(
                 probs[:, r, :],
@@ -173,15 +188,17 @@ def tile_attend_bkbetween_s_kernel(tc, keys, qpool_words, qpool_scales, ksc, qs,
                 accum_out=sums[r // 2][:, r % 2 : r % 2 + 1],
             )
 
-        slope_t = sb.tile([P, PACK, HALVES, P], F32, name="slope_t")
-        nc.vector.scalar_tensor_tensor(
-            slope_t[:].rearrange("p t h m -> p (t h m)"),
-            silu_t[:].rearrange("p t h m -> p (t h m)"),
-            -1.0,
-            gain_t[:].rearrange("p t h m -> p (t h m)"),
-            ALU.add,
-            ALU.mult,
-        )
+        factor = sb.tile([P, PACK, I], F32, name="factor", tag="neg_max1")
+        factor_banks = [bank(0), bank(1)]
+        for t in range(PACK):
+            for h in range(HALVES):
+                dst = factor_banks[t // 2][:, (t % 2) * I + h * P : (t % 2) * I + (h + 1) * P]
+                nc.tensor.matmul(dst, slope_t[:, t, h, :], ident[:], start=True, stop=False, is_transpose=True)
+                nc.tensor.matmul(
+                    dst, cols_sb[:, CHUNKS + h : CHUNKS + h + 1].to_broadcast([P, P]), ident[:], start=False, stop=True, is_transpose=True
+                )
+        for t in range(PACK):
+            nc.scalar.copy(factor[:, t, :], factor_banks[t // 2][:, (t % 2) * I : (t % 2 + 1) * I])
 
         ds_planes = sb.tile([P, PACK, I], BF16, name="ds_planes")
         for b in range(2):
@@ -202,17 +219,7 @@ def tile_attend_bkbetween_s_kernel(tc, keys, qpool_words, qpool_scales, ksc, qs,
         ds_scales = sb.tile([P, I], U8, name="ds_scales", align_bytes=64)
         nc.vector.quantize_mx(out=ds_words[:].bitcast(FP8X4), scales=ds_scales[:], in_=ds_woven[:].rearrange("p i r -> p (i r)"))
 
-        factor = [sb.tile([P, I], F32, name="factor%d" % t) for t in range(PACK)]
-        for t in range(PACK):
-            for h in range(HALVES):
-                dst = mix_banks[t][:, I + h * P : I + (h + 1) * P]
-                nc.tensor.matmul(dst, slope_t[:, t, h, :], ident[:], start=True, stop=False, is_transpose=True)
-                nc.tensor.matmul(
-                    dst, cols_sb[:, CHUNKS + h : CHUNKS + h + 1].to_broadcast([P, P]), ident[:], start=False, stop=True, is_transpose=True
-                )
-            nc.scalar.copy(factor[t][:], mix_banks[t][:, I : 2 * I])
-
-        grad_banks = [bank(4), bank(5)]
+        grad_banks = [bank(2), bank(3)]
         grads = [sb.tile([P, I], F32, name="grad%d" % t) for t in range(PACK)]
         for t in range(PACK):
             nc.tensor.matmul_mx(
@@ -227,11 +234,11 @@ def tile_attend_bkbetween_s_kernel(tc, keys, qpool_words, qpool_scales, ksc, qs,
         for t in range(PACK):
             nc.scalar.copy(grads[t][:], grad_banks[t // 2][:, (t % 2) * I : (t % 2 + 1) * I])
         for t in range(PACK):
-            nc.vector.tensor_tensor(placed[t][:].indirect(list1[:]), grads[t][:], factor[t][:], ALU.mult)
+            nc.vector.tensor_tensor(placed[t][:].indirect(list1[:]), grads[t][:], factor[:, t, :], ALU.mult)
 
         faded_t = []
         for c in range(CHUNKS):
-            turned = bank(6 + c % 2)
+            turned = bank(4 + c if c < 2 else 2 + c % 2)
             for t in range(PACK):
                 nc.tensor.transpose(
                     turned[:, t * P : (t + 1) * P], old_halves[c // 4][:, t, (c % 4) * P : (c % 4 + 1) * P], ident[:]
@@ -241,11 +248,17 @@ def tile_attend_bkbetween_s_kernel(tc, keys, qpool_words, qpool_scales, ksc, qs,
             faded_t.append(piece)
 
         out_v = out.rearrange("(p t) n -> t p n", t=PACK)
-        for t in range(PACK):
-            for h in range(2):
-                back = bank((2 * t + h) % 4)
-                for e in range(4):
-                    nc.tensor.transpose(back[:, e * P : (e + 1) * P], faded_t[4 * h + e][:, t, :], ident[:])
-                result = sb.tile([P, BANK], F32, name="result%d_%d" % (t, h))
-                nc.vector.tensor_tensor(result[:], back[:], placed[t][:, h * BANK : (h + 1) * BANK], ALU.add)
-                nc.sync.dma_start(out_v[t][:, h * BANK : (h + 1) * BANK], result[:])
+        results = sb.tile([P, PACK, T], F32, name="results", tag="neg_max1")
+        for n, (t, h) in enumerate([(3, 0), (3, 1), (0, 0), (0, 1), (1, 0), (1, 1), (2, 0), (2, 1)]):
+            back = bank((6, 7, 0, 1, 4, 5)[n % 6])
+            for e in range(4):
+                nc.tensor.transpose(back[:, e * P : (e + 1) * P], faded_t[4 * h + e][:, t, :], ident[:])
+            cols = slice(h * BANK, (h + 1) * BANK)
+            if t == PACK - 1:
+                faded = sb.tile([P, BANK], F32, name="faded_back%d" % h)
+                nc.scalar.copy(faded[:], back[:])
+                nc.gpsimd.tensor_tensor(results[:, t, cols], faded[:], placed[t][:, cols], ALU.add)
+                nc.scalar.dma_start(out_v[t][:, cols], results[:, t, cols])
+            else:
+                nc.vector.tensor_tensor(results[:, t, cols], back[:], placed[t][:, cols], ALU.add)
+                nc.sync.dma_start(out_v[t][:, cols], results[:, t, cols])

@@ -37,7 +37,7 @@ def tile_attend_bkbetween_s_kernel(tc, keys, qpool_words, qpool_scales, ksc, qs,
         list2 = sb.tile([P, I // 16], U16, name="list2")
         list4 = sb.tile([P, Q // 16], U16, name="list4")
         key_planes = [sb.tile([P, T], F32, name="keys%d" % t) for t in range(PACK)]
-        fr_rows = sb.tile([P, I], F32, name="fr_rows")
+        fr_cols = sb.tile([P, HALVES], F32, name="fr_cols")
         ksc_cols = sb.tile([P, PACK], F32, name="ksc_cols")
         qs_cols = sb.tile([P, PACK], F32, name="qs_cols")
         pool_words = sb.tile([P, U], U32, name="pool_words")
@@ -57,21 +57,21 @@ def tile_attend_bkbetween_s_kernel(tc, keys, qpool_words, qpool_scales, ksc, qs,
 
         keys_v = keys.rearrange("(p t) n -> t p n", t=PACK)
         qrows_v = qrows.rearrange("(p r) d -> p r d", r=PACK)
-        nc.sync.dma_start(list4[:], offs4)
+        nc.sync.dma_start(fr_cols[:], fr.rearrange("o (p e) -> p (o e)", e=HALVES))
         nc.sync.dma_start(list2[:], offs2)
         nc.sync.dma_start(key_planes[0][:], keys_v[0])
-        nc.sync.dma_start(fr_rows[:], fr[0].partition_broadcast(P))
-        for g in range(4):
-            nc.scalar.dma_start(pool_scales[32 * g : 32 * g + 4, :].bitcast(I32), qpool_scales[0, 4 * g : 4 * g + 4, :].bitcast(I32))
         nc.sync.dma_start(list1[:], offs)
         nc.sync.dma_start(key_planes[1][:], keys_v[1])
-        nc.sync.dma_start(qrows_raw[0][:], qrows_v[:, :, 0 : D // 2])
-        nc.sync.dma_start(key_planes[2][:], keys_v[2])
         nc.sync.dma_start(rows[0:CHUNKS, :], fade.rearrange("o (c p) -> (o c) p", p=P))
         nc.sync.dma_start(rows[CHUNKS : CHUNKS + HALVES, :], sg.rearrange("o (h p) -> (o h) p", p=P))
+        nc.sync.dma_start(key_planes[2][:], keys_v[2])
         nc.sync.dma_start(key_planes[3][:], keys_v[3])
-        nc.sync.dma_start(qrows_raw[1][:], qrows_v[:, :, D // 2 : D])
+        for g in range(4):
+            nc.sync.dma_start(pool_scales[32 * g : 32 * g + 4, :].bitcast(I32), qpool_scales[0, 4 * g : 4 * g + 4, :].bitcast(I32))
+        nc.sync.dma_start(list4[:], offs4)
         nc.sync.dma_start(pool_words[:].bitcast(I32), qpool_words[0].rearrange("p n t -> p (n t)").bitcast(I32))
+        nc.sync.dma_start(qrows_raw[0][:], qrows_v[:, :, 0 : D // 2])
+        nc.sync.dma_start(qrows_raw[1][:], qrows_v[:, :, D // 2 : D])
         nc.sync.dma_start(ksc_cols[:], ksc.rearrange("(p t) o -> p (t o)", t=PACK))
         nc.sync.dma_start(target_raw[:], target.rearrange("(p r) i -> p r i", r=PACK))
         nc.sync.dma_start(qs_cols[:], qs.rearrange("(p r) o -> p (r o)", r=PACK))
@@ -79,13 +79,14 @@ def tile_attend_bkbetween_s_kernel(tc, keys, qpool_words, qpool_scales, ksc, qs,
         for h in range(2):
             nc.sync.dma_start(old_halves[h][:], old_v[:, :, h * BANK : (h + 1) * BANK])
 
-        q_bytes = sb.tile([P, Q], U8, name="q_bytes", align_bytes=64)
-        nc.vector.tensor_copy(q_bytes[:], pool_scales[:].indirect(list4[:]))
-        q_scales = sb.tile([P, PACK, P], U8, name="q_scales", align_bytes=64)
-        nc.vector.tensor_copy(q_scales[:].rearrange("p r s -> p s r"), q_bytes[:].rearrange("p (s r) -> p s r", r=PACK))
-
         keep_rows = sb.tile([P, I], F32, name="keep_rows")
-        nc.vector.tensor_scalar(keep_rows[:], fr_rows[:], -1.0, 1.0, ALU.mult, ALU.add)
+        fr_rows = sb.tile([P, I], F32, name="fr_rows")
+        spread = bank(6)
+        for e in range(HALVES):
+            nc.tensor.transpose(spread[:, e * P : (e + 1) * P], fr_cols[:, e : e + 1].to_broadcast([P, P]), ident[:])
+        spread_v = spread[:, 0:I].rearrange("p (e s) -> p s e", e=HALVES)
+        nc.scalar.copy(fr_rows[:].rearrange("p (s e) -> p s e", e=HALVES), spread_v)
+        nc.scalar.activation(keep_rows[:].rearrange("p (s e) -> p s e", e=HALVES), spread_v, ACT.Copy, bias=1.0, scale=-1.0)
         silu_t = sb.tile([P, PACK, HALVES, P], F32, name="silu_t")
         tanh_t = sb.tile([P, PACK, HALVES, P], F32, name="tanh_t")
         mix_banks = [bank(0), bank(1)]
@@ -105,21 +106,30 @@ def tile_attend_bkbetween_s_kernel(tc, keys, qpool_words, qpool_scales, ksc, qs,
             nc.scalar.activation(tanh_t[:, t].rearrange("p h m -> p (h m)"), mix, ACT.Tanh, scale=-0.5)
             for h in range(HALVES):
                 nc.tensor.transpose(silu_banks[h][:, t * P : (t + 1) * P], silu_t[:, t, h, :], ident[:])
-            if t in (1, 2):
-                for c in range(2):
-                    m0 = (t - 1) * 64 + c * 32
-                    nc.scalar.copy(
-                        qrows_woven[:, :, m0 : m0 + 32, :].rearrange("p j m r -> p m r j"),
-                        qrows_raw[t - 1][:].rearrange("p r (m j) -> p m r j", j=PACK)[:, c * 32 : (c + 1) * 32],
-                    )
 
-        turned = bank(6)
+        turned = bank(7)
         nc.tensor.transpose(turned[:, 0:P], rows[:], ident[:])
         cols_sb = sb.tile([P, 16], F32, name="cols_sb")
         nc.scalar.copy(cols_sb[:], turned[:, 0:16])
         half_sg = sb.tile([P, HALVES], F32, name="half_sg")
         nc.scalar.activation(half_sg[:], turned[:, CHUNKS : CHUNKS + HALVES], ACT.Copy, scale=0.5)
+        fade_banks = [bank(6), bank(7)]
+        for c in range(CHUNKS):
+            nc.tensor.transpose(
+                fade_banks[c // 4][:, (c % 4) * P : (c % 4 + 1) * P], cols_sb[:, c : c + 1].to_broadcast([P, P]), ident[:]
+            )
+        factor_banks = [bank(0), bank(1)]
+        for b in range(2):
+            for n in range(4):
+                sg_col = cols_sb[:, CHUNKS + n % 2 : CHUNKS + n % 2 + 1].to_broadcast([P, P])
+                nc.tensor.matmul(
+                    factor_banks[b][:, n * P : (n + 1) * P], sg_col, ident[:], start=(n == 0), stop=False, is_transpose=True
+                )
 
+        q_bytes = sb.tile([P, Q], U8, name="q_bytes", align_bytes=64)
+        nc.vector.tensor_copy(q_bytes[:], pool_scales[:].indirect(list4[:]))
+        q_scales = sb.tile([P, PACK, P], U8, name="q_scales", align_bytes=64)
+        nc.vector.tensor_copy(q_scales[:].rearrange("p r s -> p s r"), q_bytes[:].rearrange("p (s r) -> p s r", r=PACK))
         q_words = sb.tile([P, PACK, P], U32, name="q_words", align_bytes=64)
         nc.vector.tensor_copy(q_words[:].rearrange("p r s -> p s r"), pool_words[:].indirect(list4[:]))
 
@@ -147,6 +157,11 @@ def tile_attend_bkbetween_s_kernel(tc, keys, qpool_words, qpool_scales, ksc, qs,
                 stop=True,
             )
 
+        for n in range(4):
+            nc.scalar.copy(
+                qrows_woven[:, :, n * 32 : (n + 1) * 32, :].rearrange("p j m r -> p m r j"),
+                qrows_raw[n // 2][:].rearrange("p r (m j) -> p m r j", j=PACK)[:, (n % 2) * 32 : (n % 2 + 1) * 32],
+            )
         gain_t = sb.tile([P, PACK, HALVES, P], F32, name="gain_t", align_bytes=64)
         for h in range(HALVES):
             nc.scalar.activation(
@@ -189,13 +204,15 @@ def tile_attend_bkbetween_s_kernel(tc, keys, qpool_words, qpool_scales, ksc, qs,
             )
 
         factor = sb.tile([P, PACK, I], F32, name="factor", tag="neg_max1")
-        factor_banks = [bank(0), bank(1)]
-        for t in range(PACK):
-            for h in range(HALVES):
-                dst = factor_banks[t // 2][:, (t % 2) * I + h * P : (t % 2) * I + (h + 1) * P]
-                nc.tensor.matmul(dst, slope_t[:, t, h, :], ident[:], start=True, stop=False, is_transpose=True)
+        for b in range(2):
+            for n in range(4):
                 nc.tensor.matmul(
-                    dst, cols_sb[:, CHUNKS + h : CHUNKS + h + 1].to_broadcast([P, P]), ident[:], start=False, stop=True, is_transpose=True
+                    factor_banks[b][:, n * P : (n + 1) * P],
+                    slope_t[:, 2 * b + n // 2, n % 2, :],
+                    ident[:],
+                    start=False,
+                    stop=(n == 3),
+                    is_transpose=True,
                 )
         for t in range(PACK):
             nc.scalar.copy(factor[:, t, :], factor_banks[t // 2][:, (t % 2) * I : (t % 2 + 1) * I])
@@ -219,11 +236,12 @@ def tile_attend_bkbetween_s_kernel(tc, keys, qpool_words, qpool_scales, ksc, qs,
         ds_scales = sb.tile([P, I], U8, name="ds_scales", align_bytes=64)
         nc.vector.quantize_mx(out=ds_words[:].bitcast(FP8X4), scales=ds_scales[:], in_=ds_woven[:].rearrange("p i r -> p (i r)"))
 
+        order = (PACK - 1, 0, 1, 2)
         grad_banks = [bank(2), bank(3)]
         grads = [sb.tile([P, I], F32, name="grad%d" % t) for t in range(PACK)]
-        for t in range(PACK):
+        for n, t in enumerate(order):
             nc.tensor.matmul_mx(
-                out=grad_banks[t // 2][:, (t % 2) * I : (t % 2 + 1) * I],
+                out=grad_banks[n // 2][:, (n % 2) * I : (n % 2 + 1) * I],
                 lhsT=qrows_words[:, t * P : (t + 1) * P].bitcast(FP8X4),
                 lhsT_scale=qrows_scales[:, t * P : (t + 1) * P],
                 rhs=ds_words[:].bitcast(FP8X4),
@@ -231,34 +249,37 @@ def tile_attend_bkbetween_s_kernel(tc, keys, qpool_words, qpool_scales, ksc, qs,
                 start=True,
                 stop=True,
             )
-        for t in range(PACK):
-            nc.scalar.copy(grads[t][:], grad_banks[t // 2][:, (t % 2) * I : (t % 2 + 1) * I])
-        for t in range(PACK):
+        faded_last = sb.tile([P, T], F32, name="faded_last", tag="ds_woven", align_bytes=64)
+        for h in range(2):
+            nc.vector.tensor_tensor(faded_last[:, h * BANK : (h + 1) * BANK], fade_banks[h][:], old_halves[h][:, PACK - 1, :], ALU.mult)
+        for n, t in enumerate(order):
+            nc.scalar.copy(grads[t][:], grad_banks[n // 2][:, (n % 2) * I : (n % 2 + 1) * I])
+        out_v = out.rearrange("(p t) n -> t p n", t=PACK)
+        results = sb.tile([P, PACK, T], F32, name="results")
+        for t in order:
             nc.vector.tensor_tensor(placed[t][:].indirect(list1[:]), grads[t][:], factor[:, t, :], ALU.mult)
+            if t == PACK - 1:
+                nc.vector.tensor_tensor(results[:, t, :], faded_last[:], placed[t][:], ALU.add)
+                nc.sync.dma_start(out_v[t], results[:, t, :])
 
         faded_t = []
         for c in range(CHUNKS):
             turned = bank(4 + c if c < 2 else 2 + c % 2)
-            for t in range(PACK):
+            for t in range(PACK - 1):
                 nc.tensor.transpose(
                     turned[:, t * P : (t + 1) * P], old_halves[c // 4][:, t, (c % 4) * P : (c % 4 + 1) * P], ident[:]
                 )
-            piece = sb.tile([P, PACK, P], F32, name="faded%d" % c)
-            nc.scalar.activation(piece[:].rearrange("p t m -> p (t m)"), turned[:], ACT.Copy, scale=cols_sb[:, c : c + 1])
+            piece = sb.tile([P, PACK - 1, P], F32, name="faded%d" % c)
+            nc.scalar.activation(
+                piece[:].rearrange("p t m -> p (t m)"), turned[:, 0 : (PACK - 1) * P], ACT.Copy, scale=cols_sb[:, c : c + 1]
+            )
             faded_t.append(piece)
 
-        out_v = out.rearrange("(p t) n -> t p n", t=PACK)
-        results = sb.tile([P, PACK, T], F32, name="results", tag="neg_max1")
-        for n, (t, h) in enumerate([(3, 0), (3, 1), (0, 0), (0, 1), (1, 0), (1, 1), (2, 0), (2, 1)]):
-            back = bank((6, 7, 0, 1, 4, 5)[n % 6])
-            for e in range(4):
-                nc.tensor.transpose(back[:, e * P : (e + 1) * P], faded_t[4 * h + e][:, t, :], ident[:])
+        for h in range(2):
             cols = slice(h * BANK, (h + 1) * BANK)
-            if t == PACK - 1:
-                faded = sb.tile([P, BANK], F32, name="faded_back%d" % h)
-                nc.scalar.copy(faded[:], back[:])
-                nc.gpsimd.tensor_tensor(results[:, t, cols], faded[:], placed[t][:, cols], ALU.add)
-                nc.scalar.dma_start(out_v[t][:, cols], results[:, t, cols])
-            else:
+            for t in range(PACK - 1):
+                back = bank((0, 1, 4, 5, 6, 7)[3 * h + t])
+                for e in range(4):
+                    nc.tensor.transpose(back[:, e * P : (e + 1) * P], faded_t[4 * h + e][:, t, :], ident[:])
                 nc.vector.tensor_tensor(results[:, t, cols], back[:], placed[t][:, cols], ALU.add)
                 nc.sync.dma_start(out_v[t][:, cols], results[:, t, cols])

@@ -47,12 +47,12 @@ def tile_attend_bkbetween_s_kernel(tc, keys, qpool_words, qpool_scales, ksc, qs,
         target_raw = sb.tile([P, PACK, I], F32, name="target_raw")
         old_halves = [sb.tile([P, PACK, BANK], F32, name="old%d" % h) for h in range(2)]
         ident = sb.tile([P, P], F32, name="ident")
-        placed = [sb.tile([P, T], F32, name="placed%d" % t) for t in range(PACK)]
+        placed = {t: sb.tile([P, T], F32, name="placed%d" % t) for t in (PACK - 1, 0)}
 
+        make_identity(nc, ident[:])
         nc.gpsimd.memset(pool_scales[:].bitcast(I32), 0)
         nc.vector.memset(rows[:], 0.0)
-        make_identity(nc, ident[:])
-        for t in range(PACK):
+        for t in (PACK - 1, 0):
             nc.vector.memset(placed[t][:], 0.0)
 
         keys_v = keys.rearrange("(p t) n -> t p n", t=PACK)
@@ -69,8 +69,8 @@ def tile_attend_bkbetween_s_kernel(tc, keys, qpool_words, qpool_scales, ksc, qs,
         for g in range(4):
             nc.sync.dma_start(pool_scales[32 * g : 32 * g + 4, :].bitcast(I32), qpool_scales[0, 4 * g : 4 * g + 4, :].bitcast(I32))
         nc.sync.dma_start(list4[:], offs4)
-        nc.sync.dma_start(pool_words[:].bitcast(I32), qpool_words[0].rearrange("p n t -> p (n t)").bitcast(I32))
         nc.sync.dma_start(qrows_raw[0][:], qrows_v[:, :, 0 : D // 2])
+        nc.sync.dma_start(pool_words[:].bitcast(I32), qpool_words[0].rearrange("p n t -> p (n t)").bitcast(I32))
         nc.sync.dma_start(qrows_raw[1][:], qrows_v[:, :, D // 2 : D])
         nc.sync.dma_start(ksc_cols[:], ksc.rearrange("(p t) o -> p (t o)", t=PACK))
         nc.sync.dma_start(target_raw[:], target.rearrange("(p r) i -> p r i", r=PACK))
@@ -92,6 +92,15 @@ def tile_attend_bkbetween_s_kernel(tc, keys, qpool_words, qpool_scales, ksc, qs,
         mix_banks = [bank(0), bank(1)]
         silu_banks = [bank(2), bank(3)]
         qrows_woven = sb.tile([P, PACK, P, PACK], BF16, name="qrows_woven", align_bytes=64)
+
+        def weave_qrows(half):
+            for n in range(2):
+                m0 = half * 64 + n * 32
+                nc.scalar.copy(
+                    qrows_woven[:, :, m0 : m0 + 32, :].rearrange("p j m r -> p m r j"),
+                    qrows_raw[half][:].rearrange("p r (m j) -> p m r j", j=PACK)[:, n * 32 : (n + 1) * 32],
+                )
+
         for t in range(PACK):
             second = sb.tile([P, I], F32, name="second%d" % t)
             first = sb.tile([P, I], F32, name="first%d" % t)
@@ -106,6 +115,7 @@ def tile_attend_bkbetween_s_kernel(tc, keys, qpool_words, qpool_scales, ksc, qs,
             nc.scalar.activation(tanh_t[:, t].rearrange("p h m -> p (h m)"), mix, ACT.Tanh, scale=-0.5)
             for h in range(HALVES):
                 nc.tensor.transpose(silu_banks[h][:, t * P : (t + 1) * P], silu_t[:, t, h, :], ident[:])
+        weave_qrows(0)
 
         turned = bank(7)
         nc.tensor.transpose(turned[:, 0:P], rows[:], ident[:])
@@ -157,20 +167,16 @@ def tile_attend_bkbetween_s_kernel(tc, keys, qpool_words, qpool_scales, ksc, qs,
                 stop=True,
             )
 
-        for n in range(4):
-            nc.scalar.copy(
-                qrows_woven[:, :, n * 32 : (n + 1) * 32, :].rearrange("p j m r -> p m r j"),
-                qrows_raw[n // 2][:].rearrange("p r (m j) -> p m r j", j=PACK)[:, (n % 2) * 32 : (n % 2 + 1) * 32],
-            )
-        gain_t = sb.tile([P, PACK, HALVES, P], F32, name="gain_t", align_bytes=64)
+        gain_t = sb.tile([P, PACK, HALVES, P], F32, name="gain_t")
         for h in range(HALVES):
             nc.scalar.activation(
                 gain_t[:, :, h, :], tanh_t[:, :, h, :], ACT.Identity, bias=half_sg[:, h : h + 1], scale=half_sg[:, h : h + 1]
             )
 
-        scaled_target = sb.tile([P, PACK, I], F32, name="scaled_target", tag="tanh_t")
+        weave_qrows(1)
+        scaled_target = sb.tile([P, PACK, I], F32, name="scaled_target")
         for r in range(PACK):
-            nc.scalar.activation(scaled_target[:, r, :], target_raw[:, r, :], ACT.Copy, scale=qs_cols[:, r : r + 1])
+            nc.gpsimd.tensor_scalar(scaled_target[:, r, :], target_raw[:, r, :], qs_cols[:, r : r + 1], 0.0, ALU.mult, ALU.add)
 
         slope_t = sb.tile([P, PACK, HALVES, P], F32, name="slope_t", tag="kp_woven", align_bytes=64)
         nc.vector.scalar_tensor_tensor(
@@ -182,18 +188,17 @@ def tile_attend_bkbetween_s_kernel(tc, keys, qpool_words, qpool_scales, ksc, qs,
             ALU.mult,
         )
 
-        neg_max = [sb.tile([P, 2], F32, name="neg_max%d" % b) for b in range(2)]
+        for t, tag in ((1, "silu_t"), (2, "gain_t")):
+            placed[t] = sb.tile([P, T], F32, name="placed%d" % t, tag=tag)
+            nc.gpsimd.memset(placed[t][:], 0.0)
+
+        neg_max = [sb.tile([P, 2], F32, name="neg_max%d" % b, align_bytes=64) for b in range(2)]
         sums = [sb.tile([P, 2], F32, name="sums%d" % b) for b in range(2)]
         probs = sb.tile([P, PACK, I], F32, name="probs")
         for b in range(2):
             nc.vector.tensor_reduce(
                 neg_max[b][:], score_banks[b][:].rearrange("p (r i) -> p r i", r=2), AXIS.X, ALU.max, negate=True
             )
-        qrows_words = sb.tile([P, D], U32, name="qrows_words", tag="gain_t", align_bytes=64)
-        qrows_scales = sb.tile([P, D], U8, name="qrows_scales", align_bytes=64)
-        nc.vector.quantize_mx(
-            out=qrows_words[:].bitcast(FP8X4), scales=qrows_scales[:], in_=qrows_woven[:].rearrange("p j m r -> p (j m r)")
-        )
         for r in range(PACK):
             nc.scalar.activation(
                 probs[:, r, :],
@@ -203,7 +208,7 @@ def tile_attend_bkbetween_s_kernel(tc, keys, qpool_words, qpool_scales, ksc, qs,
                 accum_out=sums[r // 2][:, r % 2 : r % 2 + 1],
             )
 
-        factor = sb.tile([P, PACK, I], F32, name="factor", tag="neg_max1")
+        factor = sb.tile([P, PACK, I], F32, name="factor", tag="neg_max1", align_bytes=64)
         for b in range(2):
             for n in range(4):
                 nc.tensor.matmul(
@@ -218,16 +223,34 @@ def tile_attend_bkbetween_s_kernel(tc, keys, qpool_words, qpool_scales, ksc, qs,
             nc.scalar.copy(factor[:, t, :], factor_banks[t // 2][:, (t % 2) * I : (t % 2 + 1) * I])
 
         ds_planes = sb.tile([P, PACK, I], BF16, name="ds_planes")
-        for b in range(2):
-            inv = sb.tile([P, 2], F32, name="inv%d" % b)
-            nc.vector.reciprocal(inv[:], sums[b][:])
-            row_scale = sb.tile([P, 2], F32, name="row_scale%d" % b)
-            nc.vector.tensor_tensor(row_scale[:], inv[:], qs_cols[:, 2 * b : 2 * b + 2], ALU.mult)
-            for e in range(2):
-                r = 2 * b + e
-                nc.vector.scalar_tensor_tensor(
-                    ds_planes[:, r, :], probs[:, r, :], row_scale[:, e : e + 1], scaled_target[:, r, :], ALU.mult, ALU.subtract
-                )
+        inv = [sb.tile([P, 2], F32, name="inv%d" % b) for b in range(2)]
+        row_scale = [sb.tile([P, 2], F32, name="row_scale%d" % b) for b in range(2)]
+
+        def scale_rows(b):
+            nc.vector.tensor_tensor(row_scale[b][:], inv[b][:], qs_cols[:, 2 * b : 2 * b + 2], ALU.mult)
+
+        def ds_plane(r):
+            nc.vector.scalar_tensor_tensor(
+                ds_planes[:, r, :],
+                probs[:, r, :],
+                row_scale[r // 2][:, r % 2 : r % 2 + 1],
+                scaled_target[:, r, :],
+                ALU.mult,
+                ALU.subtract,
+            )
+
+        nc.vector.reciprocal(inv[0][:], sums[0][:])
+        qrows_words = sb.tile([P, D], U32, name="qrows_words", tag="neg_max0", align_bytes=64)
+        qrows_scales = sb.tile([P, D], U8, name="qrows_scales", align_bytes=64)
+        nc.vector.quantize_mx(
+            out=qrows_words[:].bitcast(FP8X4), scales=qrows_scales[:], in_=qrows_woven[:].rearrange("p j m r -> p (j m r)")
+        )
+        scale_rows(0)
+        nc.vector.reciprocal(inv[1][:], sums[1][:])
+        ds_plane(0)
+        scale_rows(1)
+        for r in range(1, PACK):
+            ds_plane(r)
         ds_woven = sb.tile([P, I, PACK], BF16, name="ds_woven", align_bytes=64)
         nc.vector.tensor_copy(
             ds_woven[:].rearrange("p (c e) r -> p c r e", e=4), ds_planes[:].rearrange("p r (c e) -> p c r e", e=4)
@@ -239,9 +262,14 @@ def tile_attend_bkbetween_s_kernel(tc, keys, qpool_words, qpool_scales, ksc, qs,
         order = (PACK - 1, 0, 1, 2)
         grad_banks = [bank(2), bank(3)]
         grads = [sb.tile([P, I], F32, name="grad%d" % t) for t in range(PACK)]
-        for n, t in enumerate(order):
+        places = {PACK - 1: (0, 0), 0: (1, 0), 1: (1, 1), 2: (0, 1)}
+
+        def grad_psum(t):
+            return grad_banks[places[t][0]][:, places[t][1] * I : (places[t][1] + 1) * I]
+
+        def grad_matmul(t):
             nc.tensor.matmul_mx(
-                out=grad_banks[n // 2][:, (n % 2) * I : (n % 2 + 1) * I],
+                out=grad_psum(t),
                 lhsT=qrows_words[:, t * P : (t + 1) * P].bitcast(FP8X4),
                 lhsT_scale=qrows_scales[:, t * P : (t + 1) * P],
                 rhs=ds_words[:].bitcast(FP8X4),
@@ -249,11 +277,16 @@ def tile_attend_bkbetween_s_kernel(tc, keys, qpool_words, qpool_scales, ksc, qs,
                 start=True,
                 stop=True,
             )
+
+        for t in order[:3]:
+            grad_matmul(t)
         faded_last = sb.tile([P, T], F32, name="faded_last", tag="ds_woven", align_bytes=64)
         for h in range(2):
             nc.vector.tensor_tensor(faded_last[:, h * BANK : (h + 1) * BANK], fade_banks[h][:], old_halves[h][:, PACK - 1, :], ALU.mult)
-        for n, t in enumerate(order):
-            nc.scalar.copy(grads[t][:], grad_banks[n // 2][:, (n % 2) * I : (n % 2 + 1) * I])
+        nc.scalar.copy(grads[order[0]][:], grad_psum(order[0]))
+        grad_matmul(order[3])
+        for t in order[1:]:
+            nc.scalar.copy(grads[t][:], grad_psum(t))
         out_v = out.rearrange("(p t) n -> t p n", t=PACK)
         results = sb.tile([P, PACK, T], F32, name="results")
         for t in order:

@@ -20,11 +20,22 @@ AXIS = mybir.AxisListType
 P = 128
 PACK = 4
 BANK = 512
-HALVES = I // P
+LIST_ROWS = 16
+QUADRANT = 32
+ALIGN = 64
+SLOT_HALVES = I // P
 CHUNKS = T // P
+TOKEN_HALVES = T // BANK
+PER_BANK = BANK // P
+RUN = 4
+DIRECT = PACK - 1
+TURNED = PACK - 1
+LAST = TURNED - 1
 
 
-def tile_attend_bkbetween_s_kernel(tc, keys, qpool_words, qpool_scales, ksc, qs, target, qrows, fr, sg, old, fade, offs, offs2, offs4, out):
+def tile_attend_bkbetween_s_kernel(
+    tc, keys, qpool_words, qpool_scales, ksc, qs, target, qrows, fr, sg, old, fade, offs, offs2, offs4, out
+):
     nc = tc.nc
     with ExitStack() as ctx:
         sb = ctx.enter_context(tc.tile_pool(name="sb", bufs=1))
@@ -33,132 +44,120 @@ def tile_attend_bkbetween_s_kernel(tc, keys, qpool_words, qpool_scales, ksc, qs,
         def bank(b):
             return ps.tile([P, BANK], F32, name="bank%d" % b)
 
-        list1 = sb.tile([P, I // 16], U16, name="list1")
-        list2 = sb.tile([P, I // 16], U16, name="list2")
-        list4 = sb.tile([P, Q // 16], U16, name="list4")
+        def turn(dst, src, start, stop):
+            nc.tensor.matmul(dst, src, ident[:], start=start, stop=stop, is_transpose=True)
+
+        list1 = sb.tile([P, I // LIST_ROWS], U16, name="list1")
+        list2 = sb.tile([P, I // LIST_ROWS], U16, name="list2")
+        list4 = sb.tile([P, Q // LIST_ROWS], U16, name="list4")
         key_planes = [sb.tile([P, T], F32, name="keys%d" % t) for t in range(PACK)]
-        fr_cols = sb.tile([P, HALVES], F32, name="fr_cols")
-        ksc_cols = sb.tile([P, PACK], F32, name="ksc_cols")
+        fr_pairs = sb.tile([P, SLOT_HALVES], F32, name="fr_pairs")
+        ksc_cols = sb.tile([P, PACK], F32, name="ksc_cols", align_bytes=ALIGN)
         qs_cols = sb.tile([P, PACK], F32, name="qs_cols")
         pool_words = sb.tile([P, U], U32, name="pool_words")
         pool_scales = sb.tile([P, U], U8, name="pool_scales")
-        rows = sb.tile([P, P], F32, name="rows")
-        qrows_raw = [sb.tile([P, PACK, D // 2], F32, name="qrows_raw%d" % h) for h in range(2)]
+        vector_rows = sb.tile([P, P], F32, name="vector_rows")
+        qrows_raw = sb.tile([P, PACK, D], F32, name="qrows_raw")
         target_raw = sb.tile([P, PACK, I], F32, name="target_raw")
-        old_halves = [sb.tile([P, PACK, BANK], F32, name="old%d" % h) for h in range(2)]
+        old_halves = [sb.tile([P, PACK, BANK], F32, name="old%d" % h) for h in range(TOKEN_HALVES)]
         ident = sb.tile([P, P], F32, name="ident")
-        placed = {t: sb.tile([P, T], F32, name="placed%d" % t) for t in (PACK - 1, 0)}
+        scatter_order = (DIRECT,) + tuple(range(TURNED))
+        placed = {t: sb.tile([P, T], F32, name="placed%d" % t) for t in scatter_order[:-1]}
 
         make_identity(nc, ident[:])
         nc.gpsimd.memset(pool_scales[:].bitcast(I32), 0)
-        nc.vector.memset(rows[:], 0.0)
-        for t in (PACK - 1, 0):
+        nc.vector.memset(vector_rows[:], 0.0)
+        for t in scatter_order[:-1]:
             nc.vector.memset(placed[t][:], 0.0)
 
         keys_v = keys.rearrange("(p t) n -> t p n", t=PACK)
-        qrows_v = qrows.rearrange("(p r) d -> p r d", r=PACK)
-        nc.sync.dma_start(fr_cols[:], fr.rearrange("o (p e) -> p (o e)", e=HALVES))
+        nc.sync.dma_start(fr_pairs[:], fr.rearrange("o (p e) -> p (o e)", e=SLOT_HALVES))
         nc.sync.dma_start(list2[:], offs2)
         nc.sync.dma_start(key_planes[0][:], keys_v[0])
         nc.sync.dma_start(list1[:], offs)
         nc.sync.dma_start(key_planes[1][:], keys_v[1])
-        nc.sync.dma_start(rows[0:CHUNKS, :], fade.rearrange("o (c p) -> (o c) p", p=P))
-        nc.sync.dma_start(rows[CHUNKS : CHUNKS + HALVES, :], sg.rearrange("o (h p) -> (o h) p", p=P))
+        nc.sync.dma_start(vector_rows[0:CHUNKS, :], fade.rearrange("o (c p) -> (o c) p", p=P))
+        nc.sync.dma_start(vector_rows[CHUNKS : CHUNKS + SLOT_HALVES, :], sg.rearrange("o (h p) -> (o h) p", p=P))
         nc.sync.dma_start(key_planes[2][:], keys_v[2])
         nc.sync.dma_start(key_planes[3][:], keys_v[3])
-        for g in range(4):
-            nc.sync.dma_start(pool_scales[32 * g : 32 * g + 4, :].bitcast(I32), qpool_scales[0, 4 * g : 4 * g + 4, :].bitcast(I32))
+        for g in range(P // QUADRANT):
+            nc.sync.dma_start(
+                pool_scales[QUADRANT * g : QUADRANT * g + 4, :].bitcast(I32), qpool_scales[0, 4 * g : 4 * g + 4, :].bitcast(I32)
+            )
         nc.sync.dma_start(list4[:], offs4)
-        nc.sync.dma_start(qrows_raw[0][:], qrows_v[:, :, 0 : D // 2])
         nc.sync.dma_start(pool_words[:].bitcast(I32), qpool_words[0].rearrange("p n t -> p (n t)").bitcast(I32))
-        nc.sync.dma_start(qrows_raw[1][:], qrows_v[:, :, D // 2 : D])
         nc.sync.dma_start(ksc_cols[:], ksc.rearrange("(p t) o -> p (t o)", t=PACK))
+        nc.sync.dma_start(qrows_raw[:], qrows.rearrange("(p r) d -> p r d", r=PACK))
         nc.sync.dma_start(target_raw[:], target.rearrange("(p r) i -> p r i", r=PACK))
         nc.sync.dma_start(qs_cols[:], qs.rearrange("(p r) o -> p (r o)", r=PACK))
         old_v = old.rearrange("(p t) n -> p t n", t=PACK)
-        for h in range(2):
+        for h in range(TOKEN_HALVES):
             nc.sync.dma_start(old_halves[h][:], old_v[:, :, h * BANK : (h + 1) * BANK])
 
         keep_rows = sb.tile([P, I], F32, name="keep_rows")
         fr_rows = sb.tile([P, I], F32, name="fr_rows")
-        spread = bank(6)
-        for e in range(HALVES):
-            nc.tensor.transpose(spread[:, e * P : (e + 1) * P], fr_cols[:, e : e + 1].to_broadcast([P, P]), ident[:])
-        spread_v = spread[:, 0:I].rearrange("p (e s) -> p s e", e=HALVES)
-        nc.scalar.copy(fr_rows[:].rearrange("p (s e) -> p s e", e=HALVES), spread_v)
-        nc.scalar.activation(keep_rows[:].rearrange("p (s e) -> p s e", e=HALVES), spread_v, ACT.Copy, bias=1.0, scale=-1.0)
-        silu_t = sb.tile([P, PACK, HALVES, P], F32, name="silu_t")
-        tanh_t = sb.tile([P, PACK, HALVES, P], F32, name="tanh_t")
+        fr_bank = bank(6)
+        for e in range(SLOT_HALVES):
+            nc.tensor.transpose(fr_bank[:, e * P : (e + 1) * P], fr_pairs[:, e : e + 1].to_broadcast([P, P]), ident[:])
+        fr_in_order = fr_bank[:, 0:I].rearrange("p (e s) -> p s e", e=SLOT_HALVES)
+        nc.scalar.copy(fr_rows[:].rearrange("p (s e) -> p s e", e=SLOT_HALVES), fr_in_order)
+        nc.scalar.activation(keep_rows[:].rearrange("p (s e) -> p s e", e=SLOT_HALVES), fr_in_order, ACT.Copy, bias=1.0, scale=-1.0)
+
+        silu_t = sb.tile([P, PACK, SLOT_HALVES, P], F32, name="silu_t")
+        tanh_t = sb.tile([P, PACK, SLOT_HALVES, P], F32, name="tanh_t", align_bytes=ALIGN)
         mix_banks = [bank(0), bank(1)]
         silu_banks = [bank(2), bank(3)]
-        qrows_woven = sb.tile([P, PACK, P, PACK], BF16, name="qrows_woven", align_bytes=64)
-
-        def weave_qrows(half):
-            for n in range(2):
-                m0 = half * 64 + n * 32
-                nc.scalar.copy(
-                    qrows_woven[:, :, m0 : m0 + 32, :].rearrange("p j m r -> p m r j"),
-                    qrows_raw[half][:].rearrange("p r (m j) -> p m r j", j=PACK)[:, n * 32 : (n + 1) * 32],
-                )
-
         for t in range(PACK):
             second = sb.tile([P, I], F32, name="second%d" % t)
             first = sb.tile([P, I], F32, name="first%d" % t)
             nc.vector.tensor_tensor(second[:], key_planes[t][:].indirect(list2[:]), fr_rows[:], ALU.mult)
             nc.vector.tensor_tensor(first[:], key_planes[t][:].indirect(list1[:]), keep_rows[:], ALU.mult)
-            mix = mix_banks[t % 2][:, (t // 2) * I : (t // 2 + 1) * I]
-            for h in range(HALVES):
-                cols = slice(h * P, (h + 1) * P)
-                nc.tensor.matmul(mix[:, cols], second[:, cols], ident[:], start=True, stop=False, is_transpose=True)
-                nc.tensor.matmul(mix[:, cols], first[:, cols], ident[:], start=False, stop=True, is_transpose=True)
-            nc.scalar.activation(silu_t[:, t].rearrange("p h m -> p (h m)"), mix, ACT.Silu)
-            nc.scalar.activation(tanh_t[:, t].rearrange("p h m -> p (h m)"), mix, ACT.Tanh, scale=-0.5)
-            for h in range(HALVES):
+            mix_t = mix_banks[t % 2][:, (t // 2) * I : (t // 2 + 1) * I]
+            for h in range(SLOT_HALVES):
+                slots = slice(h * P, (h + 1) * P)
+                turn(mix_t[:, slots], second[:, slots], True, False)
+                turn(mix_t[:, slots], first[:, slots], False, True)
+            nc.scalar.activation(silu_t[:, t].rearrange("p h m -> p (h m)"), mix_t, ACT.Silu)
+            nc.scalar.activation(tanh_t[:, t].rearrange("p h m -> p (h m)"), mix_t, ACT.Tanh, scale=-0.5)
+            for h in range(SLOT_HALVES):
                 nc.tensor.transpose(silu_banks[h][:, t * P : (t + 1) * P], silu_t[:, t, h, :], ident[:])
-        weave_qrows(0)
 
-        turned = bank(7)
-        nc.tensor.transpose(turned[:, 0:P], rows[:], ident[:])
-        cols_sb = sb.tile([P, 16], F32, name="cols_sb")
-        nc.scalar.copy(cols_sb[:], turned[:, 0:16])
-        half_sg = sb.tile([P, HALVES], F32, name="half_sg")
-        nc.scalar.activation(half_sg[:], turned[:, CHUNKS : CHUNKS + HALVES], ACT.Copy, scale=0.5)
-        fade_banks = [bank(6), bank(7)]
-        for c in range(CHUNKS):
-            nc.tensor.transpose(
-                fade_banks[c // 4][:, (c % 4) * P : (c % 4 + 1) * P], cols_sb[:, c : c + 1].to_broadcast([P, P]), ident[:]
-            )
+        vector_bank = bank(7)
+        nc.tensor.transpose(vector_bank[:, 0:P], vector_rows[:], ident[:])
+        vector_cols = sb.tile([P, CHUNKS + SLOT_HALVES], F32, name="vector_cols")
+        nc.scalar.copy(vector_cols[:], vector_bank[:, 0 : CHUNKS + SLOT_HALVES])
+        half_sg = sb.tile([P, SLOT_HALVES], F32, name="half_sg")
+        nc.scalar.activation(half_sg[:], vector_bank[:, CHUNKS : CHUNKS + SLOT_HALVES], ACT.Copy, scale=0.5)
+
         factor_banks = [bank(0), bank(1)]
         for b in range(2):
-            for n in range(4):
-                sg_col = cols_sb[:, CHUNKS + n % 2 : CHUNKS + n % 2 + 1].to_broadcast([P, P])
-                nc.tensor.matmul(
-                    factor_banks[b][:, n * P : (n + 1) * P], sg_col, ident[:], start=(n == 0), stop=False, is_transpose=True
-                )
+            for n in range(PER_BANK):
+                sg_col = vector_cols[:, CHUNKS + n % SLOT_HALVES : CHUNKS + n % SLOT_HALVES + 1]
+                turn(factor_banks[b][:, n * P : (n + 1) * P], sg_col.to_broadcast([P, P]), n == 0, False)
 
-        q_bytes = sb.tile([P, Q], U8, name="q_bytes", align_bytes=64)
-        nc.vector.tensor_copy(q_bytes[:], pool_scales[:].indirect(list4[:]))
-        q_scales = sb.tile([P, PACK, P], U8, name="q_scales", align_bytes=64)
-        nc.vector.tensor_copy(q_scales[:].rearrange("p r s -> p s r"), q_bytes[:].rearrange("p (s r) -> p s r", r=PACK))
-        q_words = sb.tile([P, PACK, P], U32, name="q_words", align_bytes=64)
+        q_gathered_scales = sb.tile([P, Q], U8, name="q_gathered_scales", align_bytes=ALIGN)
+        nc.vector.tensor_copy(q_gathered_scales[:], pool_scales[:].indirect(list4[:]))
+        q_words = sb.tile([P, PACK, P], U32, name="q_words", align_bytes=ALIGN)
         nc.vector.tensor_copy(q_words[:].rearrange("p r s -> p s r"), pool_words[:].indirect(list4[:]))
 
-        kp_woven = sb.tile([P, I, PACK], BF16, name="kp_woven", align_bytes=64)
-        for h in range(HALVES):
+        kp_woven = sb.tile([P, I, PACK], BF16, name="kp_woven", align_bytes=ALIGN)
+        for h in range(SLOT_HALVES):
             nc.vector.tensor_tensor(
                 kp_woven[:, h * P : (h + 1) * P, :],
                 silu_banks[h][:].rearrange("p (t s) -> p s t", t=PACK),
                 ksc_cols[:].unsqueeze(1).to_broadcast([P, P, PACK]),
                 ALU.mult,
             )
-        kp_words = sb.tile([P, I], U32, name="kp_words", align_bytes=64)
-        kp_scales = sb.tile([P, I], U8, name="kp_scales", align_bytes=64)
+        q_scales = sb.tile([P, PACK, P], U8, name="q_scales", tag="ksc_cols", align_bytes=ALIGN)
+        nc.vector.tensor_copy(q_scales[:], q_gathered_scales[:].rearrange("p (s r) -> p r s", r=PACK))
+        kp_words = sb.tile([P, I], U32, name="kp_words", align_bytes=ALIGN)
+        kp_scales = sb.tile([P, I], U8, name="kp_scales", align_bytes=ALIGN)
         nc.vector.quantize_mx(out=kp_words[:].bitcast(FP8X4), scales=kp_scales[:], in_=kp_woven[:].rearrange("p i t -> p (i t)"))
 
-        score_banks = [bank(4), bank(5)]
+        score_banks = [bank(4 + r) for r in range(PACK)]
         for r in range(PACK):
             nc.tensor.matmul_mx(
-                out=score_banks[r // 2][:, (r % 2) * I : (r % 2 + 1) * I],
+                out=score_banks[r][:, 0:I],
                 lhsT=q_words[:, r, :].bitcast(FP8X4),
                 lhsT_scale=q_scales[:, r, :],
                 rhs=kp_words[:].bitcast(FP8X4),
@@ -167,18 +166,26 @@ def tile_attend_bkbetween_s_kernel(tc, keys, qpool_words, qpool_scales, ksc, qs,
                 stop=True,
             )
 
-        gain_t = sb.tile([P, PACK, HALVES, P], F32, name="gain_t")
-        for h in range(HALVES):
+        gain_t = sb.tile([P, PACK, SLOT_HALVES, P], F32, name="gain_t")
+        for h in range(SLOT_HALVES):
             nc.scalar.activation(
                 gain_t[:, :, h, :], tanh_t[:, :, h, :], ACT.Identity, bias=half_sg[:, h : h + 1], scale=half_sg[:, h : h + 1]
             )
 
-        weave_qrows(1)
+        def weave_qrows(pair, tag):
+            woven = sb.tile([P, 2, P, PACK], BF16, name="qrows_woven%d" % pair, tag=tag, align_bytes=ALIGN)
+            nc.scalar.copy(
+                woven[:].rearrange("p j m r -> p m r j"),
+                qrows_raw[:].rearrange("p r (m j) -> p m r j", j=PACK)[:, :, :, 2 * pair : 2 * pair + 2],
+            )
+            return woven
+
+        qrows_woven = [weave_qrows(0, "tanh_t")]
         scaled_target = sb.tile([P, PACK, I], F32, name="scaled_target")
         for r in range(PACK):
             nc.gpsimd.tensor_scalar(scaled_target[:, r, :], target_raw[:, r, :], qs_cols[:, r : r + 1], 0.0, ALU.mult, ALU.add)
 
-        slope_t = sb.tile([P, PACK, HALVES, P], F32, name="slope_t", tag="kp_woven", align_bytes=64)
+        slope_t = sb.tile([P, PACK, SLOT_HALVES, P], F32, name="slope_t", tag="kp_woven", align_bytes=ALIGN)
         nc.vector.scalar_tensor_tensor(
             slope_t[:].rearrange("p t h m -> p (t h m)"),
             silu_t[:].rearrange("p t h m -> p (t h m)"),
@@ -188,131 +195,150 @@ def tile_attend_bkbetween_s_kernel(tc, keys, qpool_words, qpool_scales, ksc, qs,
             ALU.mult,
         )
 
-        for t, tag in ((1, "silu_t"), (2, "gain_t")):
-            placed[t] = sb.tile([P, T], F32, name="placed%d" % t, tag=tag)
-            nc.gpsimd.memset(placed[t][:], 0.0)
+        placed[LAST] = sb.tile([P, T], F32, name="placed%d" % LAST, tag="silu_t")
+        nc.gpsimd.memset(placed[LAST][:], 0.0)
 
-        neg_max = [sb.tile([P, 2], F32, name="neg_max%d" % b, align_bytes=64) for b in range(2)]
-        sums = [sb.tile([P, 2], F32, name="sums%d" % b) for b in range(2)]
+        neg_max = [sb.tile([P, 2], F32, name="neg_max%d" % pair, align_bytes=ALIGN) for pair in range(2)]
+        sums = [sb.tile([P, 2], F32, name="sums%d" % pair) for pair in range(2)]
         probs = sb.tile([P, PACK, I], F32, name="probs")
-        for b in range(2):
-            nc.vector.tensor_reduce(
-                neg_max[b][:], score_banks[b][:].rearrange("p (r i) -> p r i", r=2), AXIS.X, ALU.max, negate=True
-            )
+        for r in range(PACK):
+            nc.vector.tensor_reduce(neg_max[r // 2][:, r % 2 : r % 2 + 1], score_banks[r][:, 0:I], AXIS.X, ALU.max, negate=True)
         for r in range(PACK):
             nc.scalar.activation(
                 probs[:, r, :],
-                score_banks[r // 2][:, (r % 2) * I : (r % 2 + 1) * I],
+                score_banks[r][:, 0:I],
                 ACT.Exp,
                 bias=neg_max[r // 2][:, r % 2 : r % 2 + 1],
                 accum_out=sums[r // 2][:, r % 2 : r % 2 + 1],
             )
 
-        factor = sb.tile([P, PACK, I], F32, name="factor", tag="neg_max1", align_bytes=64)
+        qrows_woven.append(weave_qrows(1, "neg_max1"))
+        factor = sb.tile([P, PACK, I], F32, name="factor", tag="qrows_raw")
         for b in range(2):
-            for n in range(4):
-                nc.tensor.matmul(
+            for n in range(PER_BANK):
+                turn(
                     factor_banks[b][:, n * P : (n + 1) * P],
-                    slope_t[:, 2 * b + n // 2, n % 2, :],
-                    ident[:],
-                    start=False,
-                    stop=(n == 3),
-                    is_transpose=True,
+                    slope_t[:, 2 * b + n // SLOT_HALVES, n % SLOT_HALVES, :],
+                    False,
+                    n == PER_BANK - 1,
                 )
-        for t in range(PACK):
-            nc.scalar.copy(factor[:, t, :], factor_banks[t // 2][:, (t % 2) * I : (t % 2 + 1) * I])
+        for b in (DIRECT // 2, 1 - DIRECT // 2):
+            nc.scalar.copy(factor[:, 2 * b : 2 * b + 2, :].rearrange("p t i -> p (t i)"), factor_banks[b][:])
 
-        ds_planes = sb.tile([P, PACK, I], BF16, name="ds_planes")
-        inv = [sb.tile([P, 2], F32, name="inv%d" % b) for b in range(2)]
-        row_scale = [sb.tile([P, 2], F32, name="row_scale%d" % b) for b in range(2)]
+        fade_banks = [bank(4), bank(5)]
+        for c in range(CHUNKS):
+            nc.tensor.transpose(
+                fade_banks[c // PER_BANK][:, (c % PER_BANK) * P : (c % PER_BANK + 1) * P],
+                vector_cols[:, c : c + 1].to_broadcast([P, P]),
+                ident[:],
+            )
 
-        def scale_rows(b):
-            nc.vector.tensor_tensor(row_scale[b][:], inv[b][:], qs_cols[:, 2 * b : 2 * b + 2], ALU.mult)
+        ds_planes = sb.tile([P, PACK, I], BF16, name="ds_planes", align_bytes=ALIGN)
+        inverse_sums = [sb.tile([P, 2], F32, name="inverse_sums%d" % pair) for pair in range(2)]
+        row_scales = [sb.tile([P, 2], F32, name="row_scales%d" % pair) for pair in range(2)]
+        qrows_words = []
+        qrows_scales = []
+
+        def scale_rows(pair):
+            nc.vector.tensor_tensor(row_scales[pair][:], inverse_sums[pair][:], qs_cols[:, 2 * pair : 2 * pair + 2], ALU.mult)
 
         def ds_plane(r):
             nc.vector.scalar_tensor_tensor(
                 ds_planes[:, r, :],
                 probs[:, r, :],
-                row_scale[r // 2][:, r % 2 : r % 2 + 1],
+                row_scales[r // 2][:, r % 2 : r % 2 + 1],
                 scaled_target[:, r, :],
                 ALU.mult,
                 ALU.subtract,
             )
 
-        nc.vector.reciprocal(inv[0][:], sums[0][:])
-        qrows_words = sb.tile([P, D], U32, name="qrows_words", tag="neg_max0", align_bytes=64)
-        qrows_scales = sb.tile([P, D], U8, name="qrows_scales", align_bytes=64)
-        nc.vector.quantize_mx(
-            out=qrows_words[:].bitcast(FP8X4), scales=qrows_scales[:], in_=qrows_woven[:].rearrange("p j m r -> p (j m r)")
-        )
+        def quantize_qrows(pair, tag):
+            words = sb.tile([P, 2 * P], U32, name="qrows_words%d" % pair, tag=tag, align_bytes=ALIGN)
+            scales = sb.tile([P, 2 * P], U8, name="qrows_scales%d" % pair, align_bytes=ALIGN)
+            nc.vector.quantize_mx(
+                out=words[:].bitcast(FP8X4), scales=scales[:], in_=qrows_woven[pair][:].rearrange("p j m r -> p (j m r)")
+            )
+            qrows_words.append(words)
+            qrows_scales.append(scales)
+
+        nc.vector.reciprocal(inverse_sums[0][:], sums[0][:])
+        quantize_qrows(0, "neg_max0")
         scale_rows(0)
-        nc.vector.reciprocal(inv[1][:], sums[1][:])
+        nc.vector.reciprocal(inverse_sums[1][:], sums[1][:])
         ds_plane(0)
         scale_rows(1)
         for r in range(1, PACK):
             ds_plane(r)
-        ds_woven = sb.tile([P, I, PACK], BF16, name="ds_woven", align_bytes=64)
+        ds_woven = sb.tile([P, I, PACK], BF16, name="ds_woven", align_bytes=ALIGN)
         nc.vector.tensor_copy(
-            ds_woven[:].rearrange("p (c e) r -> p c r e", e=4), ds_planes[:].rearrange("p r (c e) -> p c r e", e=4)
+            ds_woven[:].rearrange("p (c e) r -> p c r e", e=RUN), ds_planes[:].rearrange("p r (c e) -> p c r e", e=RUN)
         )
-        ds_words = sb.tile([P, I], U32, name="ds_words", align_bytes=64)
-        ds_scales = sb.tile([P, I], U8, name="ds_scales", align_bytes=64)
+        quantize_qrows(1, "ds_planes")
+        ds_words = sb.tile([P, I], U32, name="ds_words", align_bytes=ALIGN)
+        ds_scales = sb.tile([P, I], U8, name="ds_scales", align_bytes=ALIGN)
         nc.vector.quantize_mx(out=ds_words[:].bitcast(FP8X4), scales=ds_scales[:], in_=ds_woven[:].rearrange("p i r -> p (i r)"))
 
-        order = (PACK - 1, 0, 1, 2)
         grad_banks = [bank(2), bank(3)]
         grads = [sb.tile([P, I], F32, name="grad%d" % t) for t in range(PACK)]
-        places = {PACK - 1: (0, 0), 0: (1, 0), 1: (1, 1), 2: (0, 1)}
-
-        def grad_psum(t):
-            return grad_banks[places[t][0]][:, places[t][1] * I : (places[t][1] + 1) * I]
+        grad_psum = {
+            scatter_order[0]: grad_banks[0][:, 0:I],
+            scatter_order[1]: grad_banks[1][:, 0:I],
+            scatter_order[2]: grad_banks[1][:, I : 2 * I],
+            scatter_order[3]: grad_banks[0][:, I : 2 * I],
+        }
 
         def grad_matmul(t):
             nc.tensor.matmul_mx(
-                out=grad_psum(t),
-                lhsT=qrows_words[:, t * P : (t + 1) * P].bitcast(FP8X4),
-                lhsT_scale=qrows_scales[:, t * P : (t + 1) * P],
+                out=grad_psum[t],
+                lhsT=qrows_words[t // 2][:, (t % 2) * P : (t % 2 + 1) * P].bitcast(FP8X4),
+                lhsT_scale=qrows_scales[t // 2][:, (t % 2) * P : (t % 2 + 1) * P],
                 rhs=ds_words[:].bitcast(FP8X4),
                 rhs_scale=ds_scales[:],
                 start=True,
                 stop=True,
             )
 
-        for t in order[:3]:
+        for t in scatter_order[:-1]:
             grad_matmul(t)
-        faded_last = sb.tile([P, T], F32, name="faded_last", tag="ds_woven", align_bytes=64)
-        for h in range(2):
-            nc.vector.tensor_tensor(faded_last[:, h * BANK : (h + 1) * BANK], fade_banks[h][:], old_halves[h][:, PACK - 1, :], ALU.mult)
-        nc.scalar.copy(grads[order[0]][:], grad_psum(order[0]))
-        grad_matmul(order[3])
-        for t in order[1:]:
-            nc.scalar.copy(grads[t][:], grad_psum(t))
+        faded_direct = sb.tile([P, T], F32, name="faded_direct", tag="ds_woven", align_bytes=ALIGN)
+        for h in range(TOKEN_HALVES):
+            nc.vector.tensor_tensor(
+                faded_direct[:, h * BANK : (h + 1) * BANK], fade_banks[h][:], old_halves[h][:, DIRECT, :], ALU.mult
+            )
+        nc.scalar.copy(grads[DIRECT][:], grad_psum[DIRECT])
+        grad_matmul(LAST)
+        for t in scatter_order[1:]:
+            nc.scalar.copy(grads[t][:], grad_psum[t])
+
         out_v = out.rearrange("(p t) n -> t p n", t=PACK)
         results = sb.tile([P, PACK, T], F32, name="results")
-        for t in order:
+        for t in scatter_order:
             nc.vector.tensor_tensor(placed[t][:].indirect(list1[:]), grads[t][:], factor[:, t, :], ALU.mult)
-            if t == PACK - 1:
-                nc.vector.tensor_tensor(results[:, t, :], faded_last[:], placed[t][:], ALU.add)
+            if t == DIRECT:
+                nc.vector.tensor_tensor(results[:, t, :], faded_direct[:], placed[t][:], ALU.add)
                 nc.sync.dma_start(out_v[t], results[:, t, :])
 
         faded_t = []
         for c in range(CHUNKS):
-            turned = bank(4 + c if c < 2 else 2 + c % 2)
-            for t in range(PACK - 1):
-                nc.tensor.transpose(
-                    turned[:, t * P : (t + 1) * P], old_halves[c // 4][:, t, (c % 4) * P : (c % 4 + 1) * P], ident[:]
-                )
-            piece = sb.tile([P, PACK - 1, P], F32, name="faded%d" % c)
+            old_bank = bank(6 + c if c < 2 else 2 + c % 2)
+            for t in range(TURNED):
+                tokens = slice((c % PER_BANK) * P, (c % PER_BANK + 1) * P)
+                nc.tensor.transpose(old_bank[:, t * P : (t + 1) * P], old_halves[c // PER_BANK][:, t, tokens], ident[:])
+            chunk_t = sb.tile([P, TURNED, P], F32, name="faded%d" % c)
             nc.scalar.activation(
-                piece[:].rearrange("p t m -> p (t m)"), turned[:, 0 : (PACK - 1) * P], ACT.Copy, scale=cols_sb[:, c : c + 1]
+                chunk_t[:].rearrange("p t m -> p (t m)"), old_bank[:, 0 : TURNED * P], ACT.Copy, scale=vector_cols[:, c : c + 1]
             )
-            faded_t.append(piece)
+            faded_t.append(chunk_t)
 
-        for h in range(2):
-            cols = slice(h * BANK, (h + 1) * BANK)
-            for t in range(PACK - 1):
-                back = bank((0, 1, 4, 5, 6, 7)[3 * h + t])
-                for e in range(4):
-                    nc.tensor.transpose(back[:, e * P : (e + 1) * P], faded_t[4 * h + e][:, t, :], ident[:])
-                nc.vector.tensor_tensor(results[:, t, cols], back[:], placed[t][:, cols], ALU.add)
-                nc.sync.dma_start(out_v[t][:, cols], results[:, t, cols])
+        back_banks = (0, 1, 6, 7, 4, 5)
+        for h in range(TOKEN_HALVES):
+            for t in range(TURNED):
+                back = bank(back_banks[TURNED * h + t])
+                for e in range(PER_BANK):
+                    nc.tensor.transpose(back[:, e * P : (e + 1) * P], faded_t[PER_BANK * h + e][:, t, :], ident[:])
+                pieces = 2 if (h, t) == (TOKEN_HALVES - 1, LAST) else 1
+                width = BANK // pieces
+                for n in range(pieces):
+                    cols = slice(h * BANK + n * width, h * BANK + (n + 1) * width)
+                    nc.vector.tensor_tensor(results[:, t, cols], back[:, n * width : (n + 1) * width], placed[t][:, cols], ALU.add)
+                    nc.sync.dma_start(out_v[t][:, cols], results[:, t, cols])

from contextlib import ExitStack

import concourse.mybir as mybir
from concourse.masks import make_identity

D, T, I, Q, U = 512, 1024, 256, 512, 1024
FLOPS = 2 * Q * I * D + 2 * D * I * Q

F32 = mybir.dt.float32
BF16 = mybir.dt.bfloat16
I32 = mybir.dt.int32
U32 = mybir.dt.uint32
U16 = mybir.dt.uint16
U8 = mybir.dt.uint8
FP8X4 = mybir.dt.float8_e4m3fn_x4
ACT = mybir.ActivationFunctionType
ALU = mybir.AluOpType
AXIS = mybir.AxisListType

P = 128
PACK = 4
BANK = 512
LIST_ROWS = 16
QUADRANT = 32
ALIGN = 64
SLOT_HALVES = I // P
CHUNKS = T // P
TOKEN_HALVES = T // BANK
PER_BANK = BANK // P
RUN = 4
DIRECT = PACK - 1
TURNED = PACK - 1
LAST = TURNED - 1


def tile_attend_bkbetween_s_kernel(
    tc, keys, qpool_words, qpool_scales, ksc, qs, target, qrows, fr, sg, old, fade, offs, offs2, offs4, out
):
    nc = tc.nc
    with ExitStack() as ctx:
        sb = ctx.enter_context(tc.tile_pool(name="sb", bufs=1))
        ps = ctx.enter_context(tc.psum_pool(name="ps", bufs=1))

        def bank(b):
            return ps.tile([P, BANK], F32, name="bank%d" % b)

        def turn(dst, src, start, stop):
            nc.tensor.matmul(dst, src, ident[:], start=start, stop=stop, is_transpose=True)

        list1 = sb.tile([P, I // LIST_ROWS], U16, name="list1")
        list2 = sb.tile([P, I // LIST_ROWS], U16, name="list2")
        list4 = sb.tile([P, Q // LIST_ROWS], U16, name="list4")
        key_planes = [sb.tile([P, T], F32, name="keys%d" % t) for t in range(PACK)]
        fr_pairs = sb.tile([P, SLOT_HALVES], F32, name="fr_pairs")
        ksc_cols = sb.tile([P, PACK], F32, name="ksc_cols", align_bytes=ALIGN)
        qs_cols = sb.tile([P, PACK], F32, name="qs_cols")
        pool_words = sb.tile([P, U], U32, name="pool_words")
        pool_scales = sb.tile([P, U], U8, name="pool_scales")
        vector_rows = sb.tile([P, P], F32, name="vector_rows")
        qrows_raw = sb.tile([P, PACK, D], F32, name="qrows_raw")
        target_raw = sb.tile([P, PACK, I], F32, name="target_raw")
        old_halves = [sb.tile([P, PACK, BANK], F32, name="old%d" % h) for h in range(TOKEN_HALVES)]
        ident = sb.tile([P, P], F32, name="ident")
        scatter_order = (DIRECT,) + tuple(range(TURNED))
        placed = {t: sb.tile([P, T], F32, name="placed%d" % t) for t in scatter_order[:-1]}

        make_identity(nc, ident[:])
        nc.gpsimd.memset(pool_scales[:].bitcast(I32), 0)
        nc.vector.memset(vector_rows[:], 0.0)
        for t in scatter_order[:-1]:
            nc.vector.memset(placed[t][:], 0.0)

        keys_v = keys.rearrange("(p t) n -> t p n", t=PACK)
        nc.sync.dma_start(fr_pairs[:], fr.rearrange("o (p e) -> p (o e)", e=SLOT_HALVES))
        nc.sync.dma_start(list2[:], offs2)
        nc.sync.dma_start(key_planes[0][:], keys_v[0])
        nc.sync.dma_start(list1[:], offs)
        nc.sync.dma_start(key_planes[1][:], keys_v[1])
        nc.sync.dma_start(vector_rows[0:CHUNKS, :], fade.rearrange("o (c p) -> (o c) p", p=P))
        nc.sync.dma_start(vector_rows[CHUNKS : CHUNKS + SLOT_HALVES, :], sg.rearrange("o (h p) -> (o h) p", p=P))
        nc.sync.dma_start(key_planes[2][:], keys_v[2])
        nc.sync.dma_start(key_planes[3][:], keys_v[3])
        for g in range(P // QUADRANT):
            nc.sync.dma_start(
                pool_scales[QUADRANT * g : QUADRANT * g + 4, :].bitcast(I32), qpool_scales[0, 4 * g : 4 * g + 4, :].bitcast(I32)
            )
        nc.sync.dma_start(list4[:], offs4)
        nc.sync.dma_start(pool_words[:].bitcast(I32), qpool_words[0].rearrange("p n t -> p (n t)").bitcast(I32))
        nc.sync.dma_start(ksc_cols[:], ksc.rearrange("(p t) o -> p (t o)", t=PACK))
        nc.sync.dma_start(qrows_raw[:], qrows.rearrange("(p r) d -> p r d", r=PACK))
        nc.sync.dma_start(target_raw[:], target.rearrange("(p r) i -> p r i", r=PACK))
        nc.sync.dma_start(qs_cols[:], qs.rearrange("(p r) o -> p (r o)", r=PACK))
        old_v = old.rearrange("(p t) n -> p t n", t=PACK)
        for h in range(TOKEN_HALVES):
            nc.sync.dma_start(old_halves[h][:], old_v[:, :, h * BANK : (h + 1) * BANK])

        keep_rows = sb.tile([P, I], F32, name="keep_rows")
        fr_rows = sb.tile([P, I], F32, name="fr_rows")
        fr_bank = bank(6)
        for e in range(SLOT_HALVES):
            nc.tensor.transpose(fr_bank[:, e * P : (e + 1) * P], fr_pairs[:, e : e + 1].to_broadcast([P, P]), ident[:])
        fr_in_order = fr_bank[:, 0:I].rearrange("p (e s) -> p s e", e=SLOT_HALVES)
        nc.scalar.copy(fr_rows[:].rearrange("p (s e) -> p s e", e=SLOT_HALVES), fr_in_order)
        nc.scalar.activation(keep_rows[:].rearrange("p (s e) -> p s e", e=SLOT_HALVES), fr_in_order, ACT.Copy, bias=1.0, scale=-1.0)

        silu_t = sb.tile([P, PACK, SLOT_HALVES, P], F32, name="silu_t")
        tanh_t = sb.tile([P, PACK, SLOT_HALVES, P], F32, name="tanh_t", align_bytes=ALIGN)
        mix_banks = [bank(0), bank(1)]
        silu_banks = [bank(2), bank(3)]
        for t in range(PACK):
            second = sb.tile([P, I], F32, name="second%d" % t)
            first = sb.tile([P, I], F32, name="first%d" % t)
            nc.vector.tensor_tensor(second[:], key_planes[t][:].indirect(list2[:]), fr_rows[:], ALU.mult)
            nc.vector.tensor_tensor(first[:], key_planes[t][:].indirect(list1[:]), keep_rows[:], ALU.mult)
            mix_t = mix_banks[t % 2][:, (t // 2) * I : (t // 2 + 1) * I]
            for h in range(SLOT_HALVES):
                slots = slice(h * P, (h + 1) * P)
                turn(mix_t[:, slots], second[:, slots], True, False)
                turn(mix_t[:, slots], first[:, slots], False, True)
            nc.scalar.activation(silu_t[:, t].rearrange("p h m -> p (h m)"), mix_t, ACT.Silu)
            nc.scalar.activation(tanh_t[:, t].rearrange("p h m -> p (h m)"), mix_t, ACT.Tanh, scale=-0.5)
            for h in range(SLOT_HALVES):
                nc.tensor.transpose(silu_banks[h][:, t * P : (t + 1) * P], silu_t[:, t, h, :], ident[:])

        vector_bank = bank(7)
        nc.tensor.transpose(vector_bank[:, 0:P], vector_rows[:], ident[:])
        vector_cols = sb.tile([P, CHUNKS + SLOT_HALVES], F32, name="vector_cols")
        nc.scalar.copy(vector_cols[:], vector_bank[:, 0 : CHUNKS + SLOT_HALVES])
        half_sg = sb.tile([P, SLOT_HALVES], F32, name="half_sg")
        nc.scalar.activation(half_sg[:], vector_bank[:, CHUNKS : CHUNKS + SLOT_HALVES], ACT.Copy, scale=0.5)

        factor_banks = [bank(0), bank(1)]
        for b in range(2):
            for n in range(PER_BANK):
                sg_col = vector_cols[:, CHUNKS + n % SLOT_HALVES : CHUNKS + n % SLOT_HALVES + 1]
                turn(factor_banks[b][:, n * P : (n + 1) * P], sg_col.to_broadcast([P, P]), n == 0, False)

        q_gathered_scales = sb.tile([P, Q], U8, name="q_gathered_scales", align_bytes=ALIGN)
        nc.vector.tensor_copy(q_gathered_scales[:], pool_scales[:].indirect(list4[:]))
        q_words = sb.tile([P, PACK, P], U32, name="q_words", align_bytes=ALIGN)
        nc.vector.tensor_copy(q_words[:].rearrange("p r s -> p s r"), pool_words[:].indirect(list4[:]))

        kp_woven = sb.tile([P, I, PACK], BF16, name="kp_woven", align_bytes=ALIGN)
        for h in range(SLOT_HALVES):
            nc.vector.tensor_tensor(
                kp_woven[:, h * P : (h + 1) * P, :],
                silu_banks[h][:].rearrange("p (t s) -> p s t", t=PACK),
                ksc_cols[:].unsqueeze(1).to_broadcast([P, P, PACK]),
                ALU.mult,
            )
        q_scales = sb.tile([P, PACK, P], U8, name="q_scales", tag="ksc_cols", align_bytes=ALIGN)
        nc.vector.tensor_copy(q_scales[:], q_gathered_scales[:].rearrange("p (s r) -> p r s", r=PACK))
        kp_words = sb.tile([P, I], U32, name="kp_words", align_bytes=ALIGN)
        kp_scales = sb.tile([P, I], U8, name="kp_scales", align_bytes=ALIGN)
        nc.vector.quantize_mx(out=kp_words[:].bitcast(FP8X4), scales=kp_scales[:], in_=kp_woven[:].rearrange("p i t -> p (i t)"))

        score_banks = [bank(4 + r) for r in range(PACK)]
        for r in range(PACK):
            nc.tensor.matmul_mx(
                out=score_banks[r][:, 0:I],
                lhsT=q_words[:, r, :].bitcast(FP8X4),
                lhsT_scale=q_scales[:, r, :],
                rhs=kp_words[:].bitcast(FP8X4),
                rhs_scale=kp_scales[:],
                start=True,
                stop=True,
            )

        gain_t = sb.tile([P, PACK, SLOT_HALVES, P], F32, name="gain_t")
        for h in range(SLOT_HALVES):
            nc.scalar.activation(
                gain_t[:, :, h, :], tanh_t[:, :, h, :], ACT.Identity, bias=half_sg[:, h : h + 1], scale=half_sg[:, h : h + 1]
            )

        def weave_qrows(pair, tag):
            woven = sb.tile([P, 2, P, PACK], BF16, name="qrows_woven%d" % pair, tag=tag, align_bytes=ALIGN)
            nc.scalar.copy(
                woven[:].rearrange("p j m r -> p m r j"),
                qrows_raw[:].rearrange("p r (m j) -> p m r j", j=PACK)[:, :, :, 2 * pair : 2 * pair + 2],
            )
            return woven

        qrows_woven = [weave_qrows(0, "tanh_t")]
        scaled_target = sb.tile([P, PACK, I], F32, name="scaled_target")
        for r in range(PACK):
            nc.gpsimd.tensor_scalar(scaled_target[:, r, :], target_raw[:, r, :], qs_cols[:, r : r + 1], 0.0, ALU.mult, ALU.add)

        slope_t = sb.tile([P, PACK, SLOT_HALVES, P], F32, name="slope_t", tag="kp_woven", align_bytes=ALIGN)
        nc.vector.scalar_tensor_tensor(
            slope_t[:].rearrange("p t h m -> p (t h m)"),
            silu_t[:].rearrange("p t h m -> p (t h m)"),
            -1.0,
            gain_t[:].rearrange("p t h m -> p (t h m)"),
            ALU.add,
            ALU.mult,
        )

        placed[LAST] = sb.tile([P, T], F32, name="placed%d" % LAST, tag="silu_t")
        nc.gpsimd.memset(placed[LAST][:], 0.0)

        neg_max = [sb.tile([P, 2], F32, name="neg_max%d" % pair, align_bytes=ALIGN) for pair in range(2)]
        sums = [sb.tile([P, 2], F32, name="sums%d" % pair) for pair in range(2)]
        probs = sb.tile([P, PACK, I], F32, name="probs")
        for r in range(PACK):
            nc.vector.tensor_reduce(neg_max[r // 2][:, r % 2 : r % 2 + 1], score_banks[r][:, 0:I], AXIS.X, ALU.max, negate=True)
        for r in range(PACK):
            nc.scalar.activation(
                probs[:, r, :],
                score_banks[r][:, 0:I],
                ACT.Exp,
                bias=neg_max[r // 2][:, r % 2 : r % 2 + 1],
                accum_out=sums[r // 2][:, r % 2 : r % 2 + 1],
            )

        qrows_woven.append(weave_qrows(1, "neg_max1"))
        factor = sb.tile([P, PACK, I], F32, name="factor", tag="qrows_raw")
        for b in range(2):
            for n in range(PER_BANK):
                turn(
                    factor_banks[b][:, n * P : (n + 1) * P],
                    slope_t[:, 2 * b + n // SLOT_HALVES, n % SLOT_HALVES, :],
                    False,
                    n == PER_BANK - 1,
                )
        for b in (DIRECT // 2, 1 - DIRECT // 2):
            nc.scalar.copy(factor[:, 2 * b : 2 * b + 2, :].rearrange("p t i -> p (t i)"), factor_banks[b][:])

        fade_banks = [bank(4), bank(5)]
        for c in range(CHUNKS):
            nc.tensor.transpose(
                fade_banks[c // PER_BANK][:, (c % PER_BANK) * P : (c % PER_BANK + 1) * P],
                vector_cols[:, c : c + 1].to_broadcast([P, P]),
                ident[:],
            )

        ds_planes = sb.tile([P, PACK, I], BF16, name="ds_planes", align_bytes=ALIGN)
        inverse_sums = [sb.tile([P, 2], F32, name="inverse_sums%d" % pair) for pair in range(2)]
        row_scales = [sb.tile([P, 2], F32, name="row_scales%d" % pair) for pair in range(2)]
        qrows_words = []
        qrows_scales = []

        def scale_rows(pair):
            nc.vector.tensor_tensor(row_scales[pair][:], inverse_sums[pair][:], qs_cols[:, 2 * pair : 2 * pair + 2], ALU.mult)

        def ds_plane(r):
            nc.vector.scalar_tensor_tensor(
                ds_planes[:, r, :],
                probs[:, r, :],
                row_scales[r // 2][:, r % 2 : r % 2 + 1],
                scaled_target[:, r, :],
                ALU.mult,
                ALU.subtract,
            )

        def quantize_qrows(pair, tag):
            words = sb.tile([P, 2 * P], U32, name="qrows_words%d" % pair, tag=tag, align_bytes=ALIGN)
            scales = sb.tile([P, 2 * P], U8, name="qrows_scales%d" % pair, align_bytes=ALIGN)
            nc.vector.quantize_mx(
                out=words[:].bitcast(FP8X4), scales=scales[:], in_=qrows_woven[pair][:].rearrange("p j m r -> p (j m r)")
            )
            qrows_words.append(words)
            qrows_scales.append(scales)

        nc.vector.reciprocal(inverse_sums[0][:], sums[0][:])
        quantize_qrows(0, "neg_max0")
        scale_rows(0)
        nc.vector.reciprocal(inverse_sums[1][:], sums[1][:])
        ds_plane(0)
        scale_rows(1)
        for r in range(1, PACK):
            ds_plane(r)
        ds_woven = sb.tile([P, I, PACK], BF16, name="ds_woven", align_bytes=ALIGN)
        nc.vector.tensor_copy(
            ds_woven[:].rearrange("p (c e) r -> p c r e", e=RUN), ds_planes[:].rearrange("p r (c e) -> p c r e", e=RUN)
        )
        quantize_qrows(1, "ds_planes")
        ds_words = sb.tile([P, I], U32, name="ds_words", align_bytes=ALIGN)
        ds_scales = sb.tile([P, I], U8, name="ds_scales", align_bytes=ALIGN)
        nc.vector.quantize_mx(out=ds_words[:].bitcast(FP8X4), scales=ds_scales[:], in_=ds_woven[:].rearrange("p i r -> p (i r)"))

        grad_banks = [bank(2), bank(3)]
        grads = [sb.tile([P, I], F32, name="grad%d" % t) for t in range(PACK)]
        grad_psum = {
            scatter_order[0]: grad_banks[0][:, 0:I],
            scatter_order[1]: grad_banks[1][:, 0:I],
            scatter_order[2]: grad_banks[1][:, I : 2 * I],
            scatter_order[3]: grad_banks[0][:, I : 2 * I],
        }

        def grad_matmul(t):
            nc.tensor.matmul_mx(
                out=grad_psum[t],
                lhsT=qrows_words[t // 2][:, (t % 2) * P : (t % 2 + 1) * P].bitcast(FP8X4),
                lhsT_scale=qrows_scales[t // 2][:, (t % 2) * P : (t % 2 + 1) * P],
                rhs=ds_words[:].bitcast(FP8X4),
                rhs_scale=ds_scales[:],
                start=True,
                stop=True,
            )

        for t in scatter_order[:-1]:
            grad_matmul(t)
        faded_direct = sb.tile([P, T], F32, name="faded_direct", tag="ds_woven", align_bytes=ALIGN)
        for h in range(TOKEN_HALVES):
            nc.vector.tensor_tensor(
                faded_direct[:, h * BANK : (h + 1) * BANK], fade_banks[h][:], old_halves[h][:, DIRECT, :], ALU.mult
            )
        nc.scalar.copy(grads[DIRECT][:], grad_psum[DIRECT])
        grad_matmul(LAST)
        for t in scatter_order[1:]:
            nc.scalar.copy(grads[t][:], grad_psum[t])

        out_v = out.rearrange("(p t) n -> t p n", t=PACK)
        results = sb.tile([P, PACK, T], F32, name="results")
        for t in scatter_order:
            nc.vector.tensor_tensor(placed[t][:].indirect(list1[:]), grads[t][:], factor[:, t, :], ALU.mult)
            if t == DIRECT:
                nc.vector.tensor_tensor(results[:, t, :], faded_direct[:], placed[t][:], ALU.add)
                nc.sync.dma_start(out_v[t], results[:, t, :])

        faded_t = []
        for c in range(CHUNKS):
            old_bank = bank(6 + c if c < 2 else 2 + c % 2)
            for t in range(TURNED):
                tokens = slice((c % PER_BANK) * P, (c % PER_BANK + 1) * P)
                nc.tensor.transpose(old_bank[:, t * P : (t + 1) * P], old_halves[c // PER_BANK][:, t, tokens], ident[:])
            chunk_t = sb.tile([P, TURNED, P], F32, name="faded%d" % c)
            nc.scalar.activation(
                chunk_t[:].rearrange("p t m -> p (t m)"), old_bank[:, 0 : TURNED * P], ACT.Copy, scale=vector_cols[:, c : c + 1]
            )
            faded_t.append(chunk_t)

        back_banks = (0, 1, 6, 7, 4, 5)
        for h in range(TOKEN_HALVES):
            for t in range(TURNED):
                back = bank(back_banks[TURNED * h + t])
                for e in range(PER_BANK):
                    nc.tensor.transpose(back[:, e * P : (e + 1) * P], faded_t[PER_BANK * h + e][:, t, :], ident[:])
                pieces = 2 if (h, t) == (TOKEN_HALVES - 1, LAST) else 1
                width = BANK // pieces
                for n in range(pieces):
                    cols = slice(h * BANK + n * width, h * BANK + (n + 1) * width)
                    nc.vector.tensor_tensor(results[:, t, cols], back[:, n * width : (n + 1) * width], placed[t][:, cols], ALU.add)
                    nc.sync.dma_start(out_v[t][:, cols], results[:, t, cols])
